import numpy as np
import ml_dtypes


def mxq(x, axis, fmt="e4m3"):
    dtype, down = {"e4m3": (ml_dtypes.float8_e4m3fn, 7), "e5m2": (ml_dtypes.float8_e5m2, 14)}[fmt]
    v = np.moveaxis(np.asarray(x, np.float32).astype(ml_dtypes.bfloat16).astype(np.float64), axis, -1)
    blocks = v.reshape(v.shape[:-1] + (-1, 32))
    amax = np.abs(blocks).max(-1, keepdims=True)
    byte = np.maximum(np.where(amax > 0, np.frexp(amax)[1] - 1 + 127, 0) - down, 1)
    scale = np.exp2(byte - 127.0)
    codes = (blocks / scale).astype(np.float32).astype(dtype).astype(np.float64)
    return np.moveaxis((codes * scale).reshape(v.shape), -1, axis)


WIDE = False


def mx_kscale(k):
    if not WIDE:
        return np.ones(k)
    levels = np.array([10, -10, 5, -5, 0])
    if k % 512:
        return np.exp2(np.random.permutation(np.resize(levels, k // 32))).repeat(32)
    a = np.empty((k // 512, 16))
    for p in range(k // 512):
        a[p, :8] = np.random.permutation(np.resize(levels, 8))
        for g in range(8):
            far = levels[np.abs(levels - a[p, g]) >= 10]
            a[p, g + 8] = far[np.random.randint(len(far))]
    return np.exp2(a.ravel()).repeat(32)


def f64(x):
    return np.asarray(x).astype(np.float64)


def striped(idx):
    return np.tile(np.asarray(idx).reshape(-1, 16).T, (8, 1)).astype(np.uint16)


def unstriped(offs):
    return offs[:16].T.reshape(-1).astype(np.int64)


E2M1 = np.array([0.0, 0.5, 1.0, 1.5, 2.0, 3.0, 4.0, 6.0, -0.0, -0.5, -1.0, -1.5, -2.0, -3.0, -4.0, -6.0])


def pack_weight(w, fmt):
    k, n = w.shape
    w = f64(np.asarray(w, np.float32).astype(ml_dtypes.bfloat16)).reshape(k // 32, 32, n)
    amax = np.abs(w).max(1)
    if fmt == "e4m3":
        byte = np.frexp(amax)[1] - 1 + 127 - 7
    else:
        mant, ex = np.frexp(amax / 6.0)
        byte = np.where(mant > 0.5, ex, ex - 1) + 127
    byte = np.clip(np.where(amax > 0, byte, 1), 1, 254)
    scaled = (w * np.exp2(127.0 - byte)[:, None, :]).reshape(k, n).astype(np.float32)
    by_word = np.ascontiguousarray(scaled.reshape(k // 512, 128, 4, n).transpose(0, 1, 3, 2))
    if fmt == "e4m3":
        words = by_word.astype(ml_dtypes.float8_e4m3fn).view(np.uint8)
    else:
        c = by_word.astype(ml_dtypes.float4_e2m1fn).view(np.uint8) & 0xF
        words = (c[..., 0::2] | (c[..., 1::2] << 4)).reshape(k // 512, 128, 2 * n)
    return np.ascontiguousarray(words), np.ascontiguousarray(byte.astype(np.uint8).reshape(k // 512, 16, n))


def unpack_weight(words, scales, fmt):
    g, _, n = scales.shape
    words = np.ascontiguousarray(words).reshape(g, 128, n, -1)
    if fmt == "e4m3":
        vals = words.view(ml_dtypes.float8_e4m3fn).astype(np.float64)
    else:
        nib = np.empty((g, 128, n, 4), np.uint8)
        nib[..., 0::2] = words & 0xF
        nib[..., 1::2] = words >> 4
        vals = E2M1[nib]
    vals = vals * np.repeat(np.exp2(scales.astype(np.float64) - 127.0), 8, axis=1)[..., None]
    return vals.transpose(0, 1, 3, 2).reshape(g * 512, n)


K, T, I, F, E = 512, 2048, 512, 512, 256


def setup_inputs():
    n = np.random.standard_normal
    idx = np.random.permutation(T)[:I]
    fk = mx_kscale(K)
    ff = mx_kscale(F)
    tokp = pack_weight(n((K, T)) / fk[:, None], "e2m1")
    return {
        "tok_words": tokp[0],
        "tok_scales": tokp[1],
        "wa": (n((K, F)) * 1 / np.sqrt(K) * fk[:, None] * ff).astype(np.float32),
        "wb": (n((F, E)) * 1 / np.sqrt(F) / ff[:, None]).astype(np.float32),
        "rw": (np.random.uniform(0.2, 1.0, (1, I))).astype(np.float32),
        "res": (n((E, T)) * 0.5).astype(np.float32),
        "offs": striped(idx),
    }


def reference(tok_words, tok_scales, wa, wb, rw, res, offs):
    idx = unstriped(offs)
    toku = unpack_weight(tok_words, tok_scales, "e2m1")
    waq = mxq(f64(wa), 0, "e4m3")
    tokidxg = toku[:, idx]
    z = waq.T @ tokidxg
    h1 = np.maximum(z, 0.0)
    wbq = mxq(f64(wb), 0, "e4m3")
    h1q = mxq(h1, 0, "e4m3")
    o = wbq.T @ h1q
    x = o * f64(rw)
    xf = np.zeros((E, T))
    xf[:, idx] = x
    y = f64(res) + xf
    return y

@@ -1,0 +1,148 @@
+from contextlib import ExitStack
+
+import concourse.mybir as mybir
+from concourse.masks import make_identity
+
+K, T, I, F, E = 512, 2048, 512, 512, 256
+FLOPS = 2 * K * F * I + 2 * F * E * I
+
+F32 = mybir.dt.float32
+BF16 = mybir.dt.bfloat16
+I32 = mybir.dt.int32
+U32 = mybir.dt.uint32
+U16 = mybir.dt.uint16
+U8 = mybir.dt.uint8
+FP8X4 = mybir.dt.float8_e4m3fn_x4
+FP4X4 = mybir.dt.float4_e2m1fn_x4
+MULT = mybir.AluOpType.mult
+ADD = mybir.AluOpType.add
+MAX = mybir.AluOpType.max
+RELU = mybir.ActivationFunctionType.Relu
+COPY = mybir.ActivationFunctionType.Copy
+
+P = 128
+PACK = 4
+CHUNK = 128
+HALF = 256
+STORE_COLS = 512
+
+
+def tile_attend_depthffn_kernel(tc, tok_words, tok_scales, wa, wb, rw, res, offs, out):
+    nc = tc.nc
+    with ExitStack() as ctx:
+        held = ctx.enter_context(tc.tile_pool(name="held", bufs=1))
+        psum = ctx.enter_context(tc.psum_pool(name="psum", bufs=1))
+
+        offsets = held.tile([P, I // 16], U16, name="offsets")
+        nc.sync.dma_start(offsets[:], offs)
+        words = held.tile([P, T], U16, name="words", align_bytes=64)
+        nc.sync.dma_start(words[:].bitcast(I32), tok_words[0].bitcast(I32))
+
+        scale_rows = held.tile([P, T], U8, name="scale_rows", align_bytes=64)
+        nc.vector.memset(scale_rows[:].bitcast(I32), 0)
+        for q in range(4):
+            nc.scalar.dma_start(scale_rows[32 * q : 32 * q + 4, :].bitcast(I32), tok_scales[0, 4 * q : 4 * q + 4, :].bitcast(I32))
+
+        rw_cols = held.tile([P, PACK], F32, name="rw_cols")
+        nc.sync.dma_start(rw_cols[:], rw.rearrange("o (p c) -> (o p) c", c=PACK))
+
+        wa_rows = wa.rearrange("(p j) f -> p j f", j=PACK)
+        wa_raw = []
+        for h in range(2):
+            raw = held.tile([P, PACK, HALF], F32, name="wa_raw%d" % h)
+            nc.sync.dma_start(raw[:], wa_rows[:, :, h * HALF : (h + 1) * HALF])
+            wa_raw.append(raw)
+        wb_raw = held.tile([P, PACK, E], F32, name="wb_raw")
+        nc.sync.dma_start(wb_raw[:], wb.rearrange("(p j) e -> p j e", j=PACK))
+        res_sb = []
+        for g in range(2):
+            r = held.tile([P, T], F32, name="res%d" % g)
+            nc.sync.dma_start(r[:], res[g * P : (g + 1) * P, :])
+            res_sb.append(r)
+
+        windows = []
+        for g in range(2):
+            w = held.tile([P, T], F32, name="window%d" % g)
+            nc.vector.memset(w[:].bitcast(I32), 0)
+            windows.append(w)
+
+        ident = held.tile([P, P], F32, name="ident")
+        make_identity(nc, ident[:])
+        rw_ps = psum.tile([P, PACK, P], F32, name="rw_ps")
+        for c in range(PACK):
+            nc.tensor.transpose(rw_ps[:, c, :], rw_cols[:, c : c + 1].to_broadcast([P, P]), ident[:])
+        rw_all = held.tile([P, I], F32, name="rw_all")
+        nc.scalar.activation(rw_all[:].rearrange("p (n c) -> p n c", c=PACK), rw_ps[:].rearrange("p c n -> p n c"), COPY)
+
+        tok_codes = held.tile([P, I], U16, name="tok_codes", align_bytes=64)
+        tok_sc = held.tile([P, I], U8, name="tok_sc", align_bytes=64)
+        nc.vector.tensor_copy(tok_codes[:], words[:].indirect(offsets[:]))
+        nc.vector.tensor_copy(tok_sc[:], scale_rows[:].indirect(offsets[:]))
+
+        wa_bf = held.tile([P, PACK, P, PACK], BF16, name="wa_bf", align_bytes=64)
+        for h in range(2):
+            dst = wa_bf[:, :, h * 64 : (h + 1) * 64, :].rearrange("p t m j -> p m t j")
+            src = wa_raw[h][:].rearrange("p j (m t) -> p m t j", t=PACK)
+            if h == 0:
+                nc.scalar.copy(dst, src)
+            else:
+                nc.vector.tensor_copy(dst, src)
+        wa_codes = held.tile([P, F], U32, name="wa_codes", align_bytes=64)
+        wa_sc = held.tile([P, F], U8, name="wa_sc", align_bytes=64)
+        for t in range(PACK):
+            cols = slice(t * P, (t + 1) * P)
+            nc.vector.quantize_mx(out=wa_codes[:, cols].bitcast(FP8X4), scales=wa_sc[:, cols], in_=wa_bf[:, t, :, :].rearrange("p m j -> p (m j)"))
+
+        wb_bf = held.tile([P, E, PACK], BF16, name="wb_bf", align_bytes=64)
+        wb_codes = held.tile([P, E], U32, name="wb_codes", align_bytes=64)
+        wb_sc = held.tile([P, E], U8, name="wb_sc", align_bytes=64)
+        for g in range(2):
+            cols = slice(g * P, (g + 1) * P)
+            nc.scalar.copy(wb_bf[:, cols, :], wb_raw[:, :, cols].rearrange("p j e -> p e j"))
+            nc.vector.quantize_mx(out=wb_codes[:, cols].bitcast(FP8X4), scales=wb_sc[:, cols], in_=wb_bf[:, cols, :].rearrange("p e j -> p (e j)"))
+
+        h_bf = held.tile([P, I, PACK], BF16, name="h_bf", align_bytes=64)
+        h_codes = held.tile([P, I], U32, name="h_codes", align_bytes=64)
+        h_sc = held.tile([P, I], U8, name="h_sc", align_bytes=64)
+        for c in range(I // CHUNK):
+            slots = slice(c * CHUNK, (c + 1) * CHUNK)
+            z_ps = psum.tile([P, PACK, CHUNK], F32, name="z_ps%d" % c)
+            for t in range(PACK):
+                cols = slice(t * P, (t + 1) * P)
+                nc.tensor.matmul_mx(
+                    out=z_ps[:, t, :],
+                    lhsT=wa_codes[:, cols].bitcast(FP8X4),
+                    lhsT_scale=wa_sc[:, cols],
+                    rhs=tok_codes[:, slots].bitcast(FP4X4),
+                    rhs_scale=tok_sc[:, slots],
+                    start=True,
+                    stop=True,
+                )
+            z_view = z_ps[:].rearrange("p t n -> p n t")
+            if c == 1:
+                nc.vector.tensor_scalar_max(h_bf[:, slots, :], z_view, 0.0)
+            else:
+                nc.scalar.activation(h_bf[:, slots, :], z_view, RELU)
+            nc.vector.quantize_mx(out=h_codes[:, slots].bitcast(FP8X4), scales=h_sc[:, slots], in_=h_bf[:, slots, :].rearrange("p n t -> p (n t)"))
+
+        pieces = [(0, 0, HALF), (0, HALF, I), (1, 0, I)]
+        for n, (g, lo, hi) in enumerate(pieces):
+            cols = slice(g * P, (g + 1) * P)
+            o_ps = psum.tile([P, hi - lo], F32, name="o_ps%d" % n)
+            nc.tensor.matmul_mx(
+                out=o_ps[:],
+                lhsT=wb_codes[:, cols].bitcast(FP8X4),
+                lhsT_scale=wb_sc[:, cols],
+                rhs=h_codes[:, lo:hi].bitcast(FP8X4),
+                rhs_scale=h_sc[:, lo:hi],
+                start=True,
+                stop=True,
+            )
+            o_sb = held.tile([P, hi - lo], F32, name="o_sb%d" % n)
+            nc.scalar.copy(o_sb[:], o_ps[:])
+            nc.vector.tensor_tensor(windows[g][:].indirect(offsets[:, lo // 16 : hi // 16]), o_sb[:], rw_all[:, lo:hi], MULT)
+            if hi == I:
+                for c0 in range(0, T, STORE_COLS):
+                    tok = slice(c0, c0 + STORE_COLS)
+                    nc.vector.tensor_tensor(res_sb[g][:, tok], res_sb[g][:, tok], windows[g][:, tok], ADD)
+                    nc.sync.dma_start(out[g * P : (g + 1) * P, tok], res_sb[g][:, tok])

@@ -1,7 +1,6 @@
 from contextlib import ExitStack
 
 import concourse.mybir as mybir
-from concourse.masks import make_identity
 
 K, T, I, F, E = 512, 2048, 512, 512, 256
 FLOPS = 2 * K * F * I + 2 * F * E * I
@@ -24,7 +23,8 @@ P = 128
 PACK = 4
 CHUNK = 128
 HALF = 256
-STORE_COLS = 512
+STORE_CUTS = (0, 256, 768, 1280, 1792, 2048)
+WA_SPLIT = 88
 
 
 def tile_attend_depthffn_kernel(tc, tok_words, tok_scales, wa, wb, rw, res, offs, out):
@@ -40,35 +40,33 @@ def tile_attend_depthffn_kernel(tc, tok_words, tok_scales, wa, wb, rw, res, offs
 
         scale_rows = held.tile([P, T], U8, name="scale_rows", align_bytes=64)
         nc.vector.memset(scale_rows[:].bitcast(I32), 0)
-        for q in range(4):
-            nc.scalar.dma_start(scale_rows[32 * q : 32 * q + 4, :].bitcast(I32), tok_scales[0, 4 * q : 4 * q + 4, :].bitcast(I32))
+        scales_by_r = tok_scales[0].bitcast(I32).rearrange("(q r) c -> r q c", r=4)
+        for r in range(4):
+            nc.sync.dma_start(scale_rows[r:P:32, :].bitcast(I32), scales_by_r[r])
 
         rw_cols = held.tile([P, PACK], F32, name="rw_cols")
         nc.sync.dma_start(rw_cols[:], rw.rearrange("o (p c) -> (o p) c", c=PACK))
 
-        wa_rows = wa.rearrange("(p j) f -> p j f", j=PACK)
-        wa_raw = []
-        for h in range(2):
-            raw = held.tile([P, PACK, HALF], F32, name="wa_raw%d" % h)
-            nc.sync.dma_start(raw[:], wa_rows[:, :, h * HALF : (h + 1) * HALF])
-            wa_raw.append(raw)
-        wb_raw = held.tile([P, PACK, E], F32, name="wb_raw")
-        nc.sync.dma_start(wb_raw[:], wb.rearrange("(p j) e -> p j e", j=PACK))
-        res_sb = []
-        for g in range(2):
-            r = held.tile([P, T], F32, name="res%d" % g)
-            nc.sync.dma_start(r[:], res[g * P : (g + 1) * P, :])
-            res_sb.append(r)
+        zeros = held.tile([P, P], F32, name="zeros", tag="stage")
+        nc.gpsimd.memset(zeros[:], 0.0)
+        ident = held.tile([P, P], F32, name="ident")
+        nc.gpsimd.affine_select(out=ident[:], in_=zeros[:], compare_op=mybir.AluOpType.not_equal, fill=1.0, base=0, pattern=[[-1, P]], channel_multiplier=1)
+
+        w_raw = held.tile([P, PACK * (F + E)], F32, name="w_raw", tag="stage")
+        wa_raw = w_raw[:, : PACK * F].rearrange("p (j f) -> p j f", j=PACK)
+        wb_raw = w_raw[:, PACK * F :].rearrange("p (j e) -> p j e", j=PACK)
+        nc.sync.dma_start(wa_raw, wa.rearrange("(p j) f -> p j f", j=PACK))
+        nc.sync.dma_start(wb_raw, wb.rearrange("(p j) e -> p j e", j=PACK))
 
         windows = []
         for g in range(2):
             w = held.tile([P, T], F32, name="window%d" % g)
-            nc.vector.memset(w[:].bitcast(I32), 0)
             windows.append(w)
+        nc.vector.memset(windows[0][:].bitcast(I32), 0)
 
-        ident = held.tile([P, P], F32, name="ident")
-        make_identity(nc, ident[:])
-        rw_ps = psum.tile([P, PACK, P], F32, name="rw_ps")
+        for c0 in range(0, T, 512):
+            nc.gpsimd.memset(windows[1][:, c0 : c0 + 512], 0.0)
+        rw_ps = psum.tile([P, PACK, P], F32, name="rw_ps", tag="rw_ps")
         for c in range(PACK):
             nc.tensor.transpose(rw_ps[:, c, :], rw_cols[:, c : c + 1].to_broadcast([P, P]), ident[:])
         rw_all = held.tile([P, I], F32, name="rw_all")
@@ -79,29 +77,28 @@ def tile_attend_depthffn_kernel(tc, tok_words, tok_scales, wa, wb, rw, res, offs
         nc.vector.tensor_copy(tok_codes[:], words[:].indirect(offsets[:]))
         nc.vector.tensor_copy(tok_sc[:], scale_rows[:].indirect(offsets[:]))
 
-        wa_bf = held.tile([P, PACK, P, PACK], BF16, name="wa_bf", align_bytes=64)
-        for h in range(2):
-            dst = wa_bf[:, :, h * 64 : (h + 1) * 64, :].rearrange("p t m j -> p m t j")
-            src = wa_raw[h][:].rearrange("p j (m t) -> p m t j", t=PACK)
-            if h == 0:
-                nc.scalar.copy(dst, src)
-            else:
-                nc.vector.tensor_copy(dst, src)
+        wa_bf = held.tile([P, PACK, P, PACK], BF16, name="wa_bf", tag="weights_bf", align_bytes=64)
+        wa_dst = wa_bf[:].rearrange("p t m j -> p m t j")
+        wa_src = wa_raw.rearrange("p j (m t) -> p m t j", t=PACK)
+        nc.vector.tensor_copy(wa_dst[:, :WA_SPLIT], wa_src[:, :WA_SPLIT])
+        nc.scalar.copy(wa_dst[:, WA_SPLIT:], wa_src[:, WA_SPLIT:])
         wa_codes = held.tile([P, F], U32, name="wa_codes", align_bytes=64)
         wa_sc = held.tile([P, F], U8, name="wa_sc", align_bytes=64)
         for t in range(PACK):
             cols = slice(t * P, (t + 1) * P)
             nc.vector.quantize_mx(out=wa_codes[:, cols].bitcast(FP8X4), scales=wa_sc[:, cols], in_=wa_bf[:, t, :, :].rearrange("p m j -> p (m j)"))
 
-        wb_bf = held.tile([P, E, PACK], BF16, name="wb_bf", align_bytes=64)
+        wb_bf = held.tile([P, E, PACK], BF16, name="wb_bf", tag="weights_bf", align_bytes=64)
         wb_codes = held.tile([P, E], U32, name="wb_codes", align_bytes=64)
         wb_sc = held.tile([P, E], U8, name="wb_sc", align_bytes=64)
-        for g in range(2):
-            cols = slice(g * P, (g + 1) * P)
-            nc.scalar.copy(wb_bf[:, cols, :], wb_raw[:, :, cols].rearrange("p j e -> p e j"))
-            nc.vector.quantize_mx(out=wb_codes[:, cols].bitcast(FP8X4), scales=wb_sc[:, cols], in_=wb_bf[:, cols, :].rearrange("p e j -> p (e j)"))
+        nc.vector.tensor_copy(wb_bf[:], wb_raw.rearrange("p j e -> p e j"))
+        nc.vector.quantize_mx(out=wb_codes[:].bitcast(FP8X4), scales=wb_sc[:], in_=wb_bf[:].rearrange("p e j -> p (e j)"))
 
-        h_bf = held.tile([P, I, PACK], BF16, name="h_bf", align_bytes=64)
+        res_all = held.tile([P, 2, T], F32, name="res_all", tag="stage")
+        res_sb = [res_all[:, g, :] for g in range(2)]
+        for g in range(2):
+            nc.sync.dma_start(res_sb[g], res[g * P : (g + 1) * P, :])
+
         h_codes = held.tile([P, I], U32, name="h_codes", align_bytes=64)
         h_sc = held.tile([P, I], U8, name="h_sc", align_bytes=64)
         for c in range(I // CHUNK):
@@ -119,16 +116,14 @@ def tile_attend_depthffn_kernel(tc, tok_words, tok_scales, wa, wb, rw, res, offs
                     stop=True,
                 )
             z_view = z_ps[:].rearrange("p t n -> p n t")
-            if c == 1:
-                nc.vector.tensor_scalar_max(h_bf[:, slots, :], z_view, 0.0)
-            else:
-                nc.scalar.activation(h_bf[:, slots, :], z_view, RELU)
-            nc.vector.quantize_mx(out=h_codes[:, slots].bitcast(FP8X4), scales=h_sc[:, slots], in_=h_bf[:, slots, :].rearrange("p n t -> p (n t)"))
+            h_bf = held.tile([P, CHUNK, PACK], BF16, name="h_bf%d" % c, tag="h_bf%d" % c, align_bytes=64)
+            nc.scalar.activation(h_bf[:], z_view, RELU)
+            nc.vector.quantize_mx(out=h_codes[:, slots].bitcast(FP8X4), scales=h_sc[:, slots], in_=h_bf[:].rearrange("p n t -> p (n t)"))
 
-        pieces = [(0, 0, HALF), (0, HALF, I), (1, 0, I)]
+        pieces = [(0, 0, HALF), (1, 0, HALF), (0, HALF, I), (1, HALF, I)]
         for n, (g, lo, hi) in enumerate(pieces):
             cols = slice(g * P, (g + 1) * P)
-            o_ps = psum.tile([P, hi - lo], F32, name="o_ps%d" % n)
+            o_ps = psum.tile([P, hi - lo], F32, name="o_ps%d" % n, tag="rw_ps" if n == 3 else "o_ps%d" % n)
             nc.tensor.matmul_mx(
                 out=o_ps[:],
                 lhsT=wb_codes[:, cols].bitcast(FP8X4),
@@ -139,10 +134,15 @@ def tile_attend_depthffn_kernel(tc, tok_words, tok_scales, wa, wb, rw, res, offs
                 stop=True,
             )
             o_sb = held.tile([P, hi - lo], F32, name="o_sb%d" % n)
-            nc.scalar.copy(o_sb[:], o_ps[:])
-            nc.vector.tensor_tensor(windows[g][:].indirect(offsets[:, lo // 16 : hi // 16]), o_sb[:], rw_all[:, lo:hi], MULT)
+            places = windows[g][:].indirect(offsets[:, lo // 16 : hi // 16])
+            if n == 0:
+                nc.vector.tensor_tensor(o_sb[:], o_ps[:], rw_all[:, lo:hi], MULT)
+                nc.vector.tensor_copy(places, o_sb[:])
+            else:
+                nc.scalar.copy(o_sb[:], o_ps[:])
+                nc.vector.tensor_tensor(places, o_sb[:], rw_all[:, lo:hi], MULT)
             if hi == I:
-                for c0 in range(0, T, STORE_COLS):
-                    tok = slice(c0, c0 + STORE_COLS)
+                for c0, c1 in zip(STORE_CUTS, STORE_CUTS[1:]):
+                    tok = slice(c0, c1)
                     nc.vector.tensor_tensor(res_sb[g][:, tok], res_sb[g][:, tok], windows[g][:, tok], ADD)
                     nc.sync.dma_start(out[g * P : (g + 1) * P, tok], res_sb[g][:, tok])

@@ -15,7 +15,6 @@ FP8X4 = mybir.dt.float8_e4m3fn_x4
 FP4X4 = mybir.dt.float4_e2m1fn_x4
 MULT = mybir.AluOpType.mult
 ADD = mybir.AluOpType.add
-MAX = mybir.AluOpType.max
 RELU = mybir.ActivationFunctionType.Relu
 COPY = mybir.ActivationFunctionType.Copy
 
@@ -23,8 +22,13 @@ P = 128
 PACK = 4
 CHUNK = 128
 HALF = 256
-STORE_CUTS = (0, 256, 768, 1280, 1792, 2048)
 WA_SPLIT = 88
+GPSIMD_CUTS = (0, 256, 768, 1280)
+STORE_CUTS = (0, 256, 768, 1280, 1792, 2048)
+
+
+def mx_pass(nc, out, lhs_codes, lhs_scales, rhs_codes, rhs_scales):
+    nc.tensor.matmul_mx(out=out, lhsT=lhs_codes, lhsT_scale=lhs_scales, rhs=rhs_codes, rhs_scale=rhs_scales, start=True, stop=True)
 
 
 def tile_attend_depthffn_kernel(tc, tok_words, tok_scales, wa, wb, rw, res, offs, out):
@@ -71,6 +75,11 @@ def tile_attend_depthffn_kernel(tc, tok_words, tok_scales, wa, wb, rw, res, offs
             nc.tensor.transpose(rw_ps[:, c, :], rw_cols[:, c : c + 1].to_broadcast([P, P]), ident[:])
         rw_all = held.tile([P, I], F32, name="rw_all")
         nc.scalar.activation(rw_all[:].rearrange("p (n c) -> p n c", c=PACK), rw_ps[:].rearrange("p c n -> p n c"), COPY)
+        rw_turned = psum.tile([P, I // CHUNK, P], F32, name="rw_turned", tag="rw_ps")
+        for c in range(I // CHUNK):
+            nc.tensor.transpose(rw_turned[:, c, :], rw_all[:, c * CHUNK : (c + 1) * CHUNK], ident[:])
+        rw_slot = held.tile([P, I // CHUNK], F32, name="rw_slot")
+        nc.scalar.copy(rw_slot[:], rw_turned[:, :, 0])
 
         tok_codes = held.tile([P, I], U16, name="tok_codes", align_bytes=64)
         tok_sc = held.tile([P, I], U8, name="tok_sc", align_bytes=64)
@@ -95,54 +104,54 @@ def tile_attend_depthffn_kernel(tc, tok_words, tok_scales, wa, wb, rw, res, offs
         nc.vector.quantize_mx(out=wb_codes[:].bitcast(FP8X4), scales=wb_sc[:], in_=wb_bf[:].rearrange("p e j -> p (e j)"))
 
         res_all = held.tile([P, 2, T], F32, name="res_all", tag="stage")
-        res_sb = [res_all[:, g, :] for g in range(2)]
         for g in range(2):
-            nc.sync.dma_start(res_sb[g], res[g * P : (g + 1) * P, :])
+            nc.sync.dma_start(res_all[:, g, :], res[g * P : (g + 1) * P, :])
 
         h_codes = held.tile([P, I], U32, name="h_codes", align_bytes=64)
         h_sc = held.tile([P, I], U8, name="h_sc", align_bytes=64)
         for c in range(I // CHUNK):
             slots = slice(c * CHUNK, (c + 1) * CHUNK)
-            z_ps = psum.tile([P, PACK, CHUNK], F32, name="z_ps%d" % c)
+            z_ps = psum.tile([P, PACK, CHUNK], F32, name="z_ps%d" % c, tag="bank%d" % c)
             for t in range(PACK):
                 cols = slice(t * P, (t + 1) * P)
-                nc.tensor.matmul_mx(
-                    out=z_ps[:, t, :],
-                    lhsT=wa_codes[:, cols].bitcast(FP8X4),
-                    lhsT_scale=wa_sc[:, cols],
-                    rhs=tok_codes[:, slots].bitcast(FP4X4),
-                    rhs_scale=tok_sc[:, slots],
-                    start=True,
-                    stop=True,
-                )
-            z_view = z_ps[:].rearrange("p t n -> p n t")
-            h_bf = held.tile([P, CHUNK, PACK], BF16, name="h_bf%d" % c, tag="h_bf%d" % c, align_bytes=64)
-            nc.scalar.activation(h_bf[:], z_view, RELU)
+                mx_pass(nc, z_ps[:, t, :], wa_codes[:, cols].bitcast(FP8X4), wa_sc[:, cols], tok_codes[:, slots].bitcast(FP4X4), tok_sc[:, slots])
+            h_bf = held.tile([P, CHUNK, PACK], BF16, name="h_bf%d" % c, align_bytes=64)
+            nc.scalar.activation(h_bf[:], z_ps[:].rearrange("p t n -> p n t"), RELU)
             nc.vector.quantize_mx(out=h_codes[:, slots].bitcast(FP8X4), scales=h_sc[:, slots], in_=h_bf[:].rearrange("p n t -> p (n t)"))
 
-        pieces = [(0, 0, HALF), (1, 0, HALF), (0, HALF, I), (1, HALF, I)]
-        for n, (g, lo, hi) in enumerate(pieces):
-            cols = slice(g * P, (g + 1) * P)
-            o_ps = psum.tile([P, hi - lo], F32, name="o_ps%d" % n, tag="rw_ps" if n == 3 else "o_ps%d" % n)
-            nc.tensor.matmul_mx(
-                out=o_ps[:],
-                lhsT=wb_codes[:, cols].bitcast(FP8X4),
-                lhsT_scale=wb_sc[:, cols],
-                rhs=h_codes[:, lo:hi].bitcast(FP8X4),
-                rhs_scale=h_sc[:, lo:hi],
-                start=True,
-                stop=True,
-            )
-            o_sb = held.tile([P, hi - lo], F32, name="o_sb%d" % n)
-            places = windows[g][:].indirect(offsets[:, lo // 16 : hi // 16])
-            if n == 0:
-                nc.vector.tensor_tensor(o_sb[:], o_ps[:], rw_all[:, lo:hi], MULT)
-                nc.vector.tensor_copy(places, o_sb[:])
-            else:
-                nc.scalar.copy(o_sb[:], o_ps[:])
-                nc.vector.tensor_tensor(places, o_sb[:], rw_all[:, lo:hi], MULT)
-            if hi == I:
-                for c0, c1 in zip(STORE_CUTS, STORE_CUTS[1:]):
-                    tok = slice(c0, c1)
-                    nc.vector.tensor_tensor(res_sb[g][:, tok], res_sb[g][:, tok], windows[g][:, tok], ADD)
-                    nc.sync.dma_start(out[g * P : (g + 1) * P, tok], res_sb[g][:, tok])
+        for h in range(2):
+            slots = slice(h * HALF, (h + 1) * HALF)
+            o_ps = psum.tile([P, HALF], F32, name="o_ps%d" % h)
+            mx_pass(nc, o_ps[:], wb_codes[:, :P].bitcast(FP8X4), wb_sc[:, :P], h_codes[:, slots].bitcast(FP8X4), h_sc[:, slots])
+            o_sb = held.tile([P, HALF], F32, name="o_sb%d" % h)
+            places = windows[0][:].indirect(offsets[:, h * HALF // 16 : (h + 1) * HALF // 16])
+            nc.scalar.copy(o_sb[:], o_ps[:])
+            nc.vector.tensor_tensor(places, o_sb[:], rw_all[:, slots], MULT)
+
+        x_high = held.tile([P, I], F32, name="x_high", tag="x_high")
+        for h in range(2):
+            turned_ps = psum.tile([P, 2, P], F32, name="turned_ps%d" % h, tag="bank%d" % (2 * h))
+            turned = held.tile([P, 2, P], F32, name="turned%d" % h)
+            back_ps = psum.tile([P, 2, CHUNK], F32, name="back_ps%d" % h, tag="bank%d" % (2 * h + 1))
+            for u in range(2):
+                slots = slice((2 * h + u) * CHUNK, (2 * h + u + 1) * CHUNK)
+                mx_pass(nc, turned_ps[:, u, :], h_codes[:, slots].bitcast(FP8X4), h_sc[:, slots], wb_codes[:, P:].bitcast(FP8X4), wb_sc[:, P:])
+            for u in range(2):
+                nc.scalar.activation(turned[:, u, :], turned_ps[:, u, :], COPY, scale=rw_slot[:, 2 * h + u : 2 * h + u + 1])
+            for u in range(2):
+                nc.tensor.transpose(back_ps[:, u, :], turned[:, u, :], ident[:])
+            nc.scalar.copy(x_high[:, h * HALF : (h + 1) * HALF], back_ps[:].rearrange("p u n -> p (u n)"))
+        nc.vector.tensor_copy(windows[1][:].indirect(offsets[:]), x_high[:])
+
+        for c0, c1 in zip(GPSIMD_CUTS, GPSIMD_CUTS[1:]):
+            nc.gpsimd.tensor_tensor(res_all[:, 0, c0:c1], res_all[:, 0, c0:c1], windows[0][:, c0:c1], ADD)
+            nc.sync.dma_start(out[:P, c0:c1], res_all[:, 0, c0:c1])
+        rest = GPSIMD_CUTS[-1]
+        low_rest = held.tile([P, T - rest], F32, name="low_rest", tag="x_high")
+        nc.vector.tensor_tensor(low_rest[:, :256], res_all[:, 0, rest : rest + 256], windows[0][:, rest : rest + 256], ADD)
+        nc.sync.dma_start(out[:P, rest : rest + 256], low_rest[:, :256])
+        nc.vector.tensor_tensor(low_rest[:, 256:], res_all[:, 0, rest + 256 :], windows[0][:, rest + 256 :], ADD)
+        nc.sync.dma_start(out[:P, rest + 256 :], low_rest[:, 256:])
+        for c0, c1 in zip(STORE_CUTS, STORE_CUTS[1:]):
+            nc.vector.tensor_tensor(res_all[:, 1, c0:c1], res_all[:, 1, c0:c1], windows[1][:, c0:c1], ADD)
+            nc.sync.dma_start(out[P:, c0:c1], res_all[:, 1, c0:c1])

@@ -23,7 +23,7 @@ PACK = 4
 CHUNK = 128
 HALF = 256
 WA_SPLIT = 88
-GPSIMD_CUTS = (0, 256, 768, 1280)
+GPSIMD_CUTS = (0, 384, 896, 1280)
 STORE_CUTS = (0, 256, 768, 1280, 1792, 2048)
 
 
@@ -66,7 +66,8 @@ def tile_attend_depthffn_kernel(tc, tok_words, tok_scales, wa, wb, rw, res, offs
         for g in range(2):
             w = held.tile([P, T], F32, name="window%d" % g)
             windows.append(w)
-        nc.vector.memset(windows[0][:].bitcast(I32), 0)
+        for c0 in range(0, T, T // 2):
+            nc.vector.memset(windows[0][:, c0 : c0 + T // 2].bitcast(I32), 0)
 
         for c0 in range(0, T, 512):
             nc.gpsimd.memset(windows[1][:, c0 : c0 + 512], 0.0)
@@ -103,9 +104,10 @@ def tile_attend_depthffn_kernel(tc, tok_words, tok_scales, wa, wb, rw, res, offs
         nc.vector.tensor_copy(wb_bf[:], wb_raw.rearrange("p j e -> p e j"))
         nc.vector.quantize_mx(out=wb_codes[:].bitcast(FP8X4), scales=wb_sc[:], in_=wb_bf[:].rearrange("p e j -> p (e j)"))
 
-        res_all = held.tile([P, 2, T], F32, name="res_all", tag="stage")
-        for g in range(2):
-            nc.sync.dma_start(res_all[:, g, :], res[g * P : (g + 1) * P, :])
+        res_low = held.tile([P, T], F32, name="res_low", tag="stage")
+        nc.sync.dma_start(res_low[:], res[:P, :])
+        res_high = held.tile([P, T], F32, name="res_high", tag="weights_bf", align_bytes=64)
+        nc.sync.dma_start(res_high[:], res[P:, :])
 
         h_codes = held.tile([P, I], U32, name="h_codes", align_bytes=64)
         h_sc = held.tile([P, I], U8, name="h_sc", align_bytes=64)
@@ -115,43 +117,57 @@ def tile_attend_depthffn_kernel(tc, tok_words, tok_scales, wa, wb, rw, res, offs
             for t in range(PACK):
                 cols = slice(t * P, (t + 1) * P)
                 mx_pass(nc, z_ps[:, t, :], wa_codes[:, cols].bitcast(FP8X4), wa_sc[:, cols], tok_codes[:, slots].bitcast(FP4X4), tok_sc[:, slots])
-            h_bf = held.tile([P, CHUNK, PACK], BF16, name="h_bf%d" % c, align_bytes=64)
-            nc.scalar.activation(h_bf[:], z_ps[:].rearrange("p t n -> p n t"), RELU)
+            h_bf = held.tile([P, CHUNK, PACK], BF16, name="h_bf%d" % c, tag="h_bf%d" % (c if c < 3 else 1), align_bytes=64)
+            if c < 3:
+                nc.scalar.activation(h_bf[:], z_ps[:].rearrange("p t n -> p n t"), RELU)
+            else:
+                nc.vector.tensor_scalar_max(h_bf[:], z_ps[:].rearrange("p t n -> p n t"), 0.0)
             nc.vector.quantize_mx(out=h_codes[:, slots].bitcast(FP8X4), scales=h_sc[:, slots], in_=h_bf[:].rearrange("p n t -> p (n t)"))
 
         for h in range(2):
             slots = slice(h * HALF, (h + 1) * HALF)
-            o_ps = psum.tile([P, HALF], F32, name="o_ps%d" % h)
+            o_ps = psum.tile([P, HALF], F32, name="o_ps%d" % h, tag="o_ps%d" % h)
             mx_pass(nc, o_ps[:], wb_codes[:, :P].bitcast(FP8X4), wb_sc[:, :P], h_codes[:, slots].bitcast(FP8X4), h_sc[:, slots])
             o_sb = held.tile([P, HALF], F32, name="o_sb%d" % h)
             places = windows[0][:].indirect(offsets[:, h * HALF // 16 : (h + 1) * HALF // 16])
             nc.scalar.copy(o_sb[:], o_ps[:])
             nc.vector.tensor_tensor(places, o_sb[:], rw_all[:, slots], MULT)
 
-        x_high = held.tile([P, I], F32, name="x_high", tag="x_high")
+        x_high = held.tile([P, I], F32, name="x_high")
         for h in range(2):
             turned_ps = psum.tile([P, 2, P], F32, name="turned_ps%d" % h, tag="bank%d" % (2 * h))
             turned = held.tile([P, 2, P], F32, name="turned%d" % h)
-            back_ps = psum.tile([P, 2, CHUNK], F32, name="back_ps%d" % h, tag="bank%d" % (2 * h + 1))
             for u in range(2):
                 slots = slice((2 * h + u) * CHUNK, (2 * h + u + 1) * CHUNK)
                 mx_pass(nc, turned_ps[:, u, :], h_codes[:, slots].bitcast(FP8X4), h_sc[:, slots], wb_codes[:, P:].bitcast(FP8X4), wb_sc[:, P:])
             for u in range(2):
                 nc.scalar.activation(turned[:, u, :], turned_ps[:, u, :], COPY, scale=rw_slot[:, 2 * h + u : 2 * h + u + 1])
             for u in range(2):
-                nc.tensor.transpose(back_ps[:, u, :], turned[:, u, :], ident[:])
-            nc.scalar.copy(x_high[:, h * HALF : (h + 1) * HALF], back_ps[:].rearrange("p u n -> p (u n)"))
+                back_ps = psum.tile([P, CHUNK], F32, name="back_ps%d%d" % (h, u), tag="bank%d" % (2 * u + 1))
+                nc.tensor.transpose(back_ps[:], turned[:, u, :], ident[:])
+                nc.scalar.copy(x_high[:, (2 * h + u) * CHUNK : (2 * h + u + 1) * CHUNK], back_ps[:])
         nc.vector.tensor_copy(windows[1][:].indirect(offsets[:]), x_high[:])
 
+        out_low = held.tile([P, GPSIMD_CUTS[-1]], F32, name="out_low")
         for c0, c1 in zip(GPSIMD_CUTS, GPSIMD_CUTS[1:]):
-            nc.gpsimd.tensor_tensor(res_all[:, 0, c0:c1], res_all[:, 0, c0:c1], windows[0][:, c0:c1], ADD)
-            nc.sync.dma_start(out[:P, c0:c1], res_all[:, 0, c0:c1])
-        rest = GPSIMD_CUTS[-1]
-        low_rest = held.tile([P, T - rest], F32, name="low_rest", tag="x_high")
-        nc.vector.tensor_tensor(low_rest[:, :256], res_all[:, 0, rest : rest + 256], windows[0][:, rest : rest + 256], ADD)
-        nc.sync.dma_start(out[:P, rest : rest + 256], low_rest[:, :256])
-        nc.vector.tensor_tensor(low_rest[:, 256:], res_all[:, 0, rest + 256 :], windows[0][:, rest + 256 :], ADD)
-        nc.sync.dma_start(out[:P, rest + 256 :], low_rest[:, 256:])
+            nc.gpsimd.tensor_tensor(out_low[:, c0:c1], res_low[:, c0:c1], windows[0][:, c0:c1], ADD)
+            nc.sync.dma_start(out[:P, c0:c1], out_low[:, c0:c1])
+        for u in range(3):
+            first = GPSIMD_CUTS[-1] + u * 2 * P
+            sum_ps = psum.tile([P, 2, P], F32, name="sum_ps%d" % u, tag="bank%d" % (2 * (u % 2) + 1))
+            for b in range(2):
+                tok = slice(first + b * P, first + (b + 1) * P)
+                nc.tensor.matmul(sum_ps[:, b, :], res_low[:, tok], ident[:], start=True, stop=False, is_transpose=True)
+                nc.tensor.matmul(sum_ps[:, b, :], windows[0][:, tok], ident[:], start=False, stop=True, is_transpose=True)
+            sum_turned = held.tile([P, 2, P], F32, name="sum_turned%d" % u)
+            nc.scalar.copy(sum_turned[:], sum_ps[:])
+            sum_back = psum.tile([P, 2, P], F32, name="sum_back%d" % u, tag="o_ps%d" % (u % 2))
+            for b in range(2):
+                nc.tensor.transpose(sum_back[:, b, :], sum_turned[:, b, :], ident[:])
+            sum_sb = held.tile([P, 2 * P], F32, name="sum_sb%d" % u)
+            nc.scalar.copy(sum_sb[:], sum_back[:].rearrange("p b n -> p (b n)"))
+            nc.scalar.dma_start(out[:P, first : first + 2 * P], sum_sb[:])
+        out_high = held.tile([P, T], F32, name="out_high", tag="stage")
         for c0, c1 in zip(STORE_CUTS, STORE_CUTS[1:]):
-            nc.vector.tensor_tensor(res_all[:, 1, c0:c1], res_all[:, 1, c0:c1], windows[1][:, c0:c1], ADD)
-            nc.sync.dma_start(out[P:, c0:c1], res_all[:, 1, c0:c1])
+            nc.vector.tensor_tensor(out_high[:, c0:c1], res_high[:, c0:c1], windows[1][:, c0:c1], ADD)
+            nc.sync.dma_start(out[P:, c0:c1], out_high[:, c0:c1])

@@ -38,9 +38,9 @@ def tile_attend_depthffn_kernel(tc, tok_words, tok_scales, wa, wb, rw, res, offs
         psum = ctx.enter_context(tc.psum_pool(name="psum", bufs=1))
 
         offsets = held.tile([P, I // 16], U16, name="offsets")
-        nc.sync.dma_start(offsets[:], offs)
         words = held.tile([P, T], U16, name="words", align_bytes=64)
         nc.sync.dma_start(words[:].bitcast(I32), tok_words[0].bitcast(I32))
+        nc.sync.dma_start(offsets[:], offs)
 
         scale_rows = held.tile([P, T], U8, name="scale_rows", align_bytes=64)
         nc.vector.memset(scale_rows[:].bitcast(I32), 0)
@@ -66,11 +66,10 @@ def tile_attend_depthffn_kernel(tc, tok_words, tok_scales, wa, wb, rw, res, offs
         for g in range(2):
             w = held.tile([P, T], F32, name="window%d" % g)
             windows.append(w)
-        for c0 in range(0, T, T // 2):
-            nc.vector.memset(windows[0][:, c0 : c0 + T // 2].bitcast(I32), 0)
-
-        for c0 in range(0, T, 512):
-            nc.gpsimd.memset(windows[1][:, c0 : c0 + 512], 0.0)
+        for c0 in (0, 512):
+            nc.vector.memset(windows[0][:, c0 : c0 + 512].bitcast(I32), 0)
+        for g, c0 in [(0, 1024), (0, 1536), (1, 0), (1, 512), (1, 1024), (1, 1536)]:
+            nc.gpsimd.memset(windows[g][:, c0 : c0 + 512], 0.0)
         rw_ps = psum.tile([P, PACK, P], F32, name="rw_ps", tag="rw_ps")
         for c in range(PACK):
             nc.tensor.transpose(rw_ps[:, c, :], rw_cols[:, c : c + 1].to_broadcast([P, P]), ident[:])

@@ -23,7 +23,7 @@ PACK = 4
 CHUNK = 128
 HALF = 256
 WA_SPLIT = 88
-GPSIMD_CUTS = (0, 384, 896, 1280)
+GPSIMD_CUTS = (0, 640, 1152)
 STORE_CUTS = (0, 256, 768, 1280, 1792, 2048)
 
 
@@ -35,6 +35,7 @@ def tile_attend_depthffn_kernel(tc, tok_words, tok_scales, wa, wb, rw, res, offs
     nc = tc.nc
     with ExitStack() as ctx:
         held = ctx.enter_context(tc.tile_pool(name="held", bufs=1))
+        shared = ctx.enter_context(tc.tile_pool(name="shared", bufs=1))
         psum = ctx.enter_context(tc.psum_pool(name="psum", bufs=1))
 
         offsets = held.tile([P, I // 16], U16, name="offsets")
@@ -42,21 +43,23 @@ def tile_attend_depthffn_kernel(tc, tok_words, tok_scales, wa, wb, rw, res, offs
         nc.sync.dma_start(words[:].bitcast(I32), tok_words[0].bitcast(I32))
         nc.sync.dma_start(offsets[:], offs)
 
+        rw_cols = held.tile([P, PACK], F32, name="rw_cols")
+        nc.scalar.dma_start(rw_cols[:], rw.rearrange("o (p c) -> (o p) c", c=PACK))
+
         scale_rows = held.tile([P, T], U8, name="scale_rows", align_bytes=64)
-        nc.vector.memset(scale_rows[:].bitcast(I32), 0)
+        nc.gpsimd.memset(scale_rows[:].bitcast(I32), 0)
         scales_by_r = tok_scales[0].bitcast(I32).rearrange("(q r) c -> r q c", r=4)
         for r in range(4):
-            nc.sync.dma_start(scale_rows[r:P:32, :].bitcast(I32), scales_by_r[r])
+            queue = nc.sync if r < 2 else nc.scalar
+            queue.dma_start(scale_rows[r:P:32, :].bitcast(I32), scales_by_r[r])
 
-        rw_cols = held.tile([P, PACK], F32, name="rw_cols")
-        nc.sync.dma_start(rw_cols[:], rw.rearrange("o (p c) -> (o p) c", c=PACK))
 
-        zeros = held.tile([P, P], F32, name="zeros", tag="stage")
-        nc.gpsimd.memset(zeros[:], 0.0)
+        zeros = shared.tile([P, P], F32, name="zeros", offset=0)
+        nc.vector.memset(zeros[:], 0.0)
         ident = held.tile([P, P], F32, name="ident")
         nc.gpsimd.affine_select(out=ident[:], in_=zeros[:], compare_op=mybir.AluOpType.not_equal, fill=1.0, base=0, pattern=[[-1, P]], channel_multiplier=1)
 
-        w_raw = held.tile([P, PACK * (F + E)], F32, name="w_raw", tag="stage")
+        w_raw = shared.tile([P, PACK * (F + E)], F32, name="w_raw", offset=0)
         wa_raw = w_raw[:, : PACK * F].rearrange("p (j f) -> p j f", j=PACK)
         wb_raw = w_raw[:, PACK * F :].rearrange("p (j e) -> p j e", j=PACK)
         nc.sync.dma_start(wa_raw, wa.rearrange("(p j) f -> p j f", j=PACK))
@@ -66,9 +69,9 @@ def tile_attend_depthffn_kernel(tc, tok_words, tok_scales, wa, wb, rw, res, offs
         for g in range(2):
             w = held.tile([P, T], F32, name="window%d" % g)
             windows.append(w)
-        for c0 in (0, 512):
+        for c0 in (0, 512, 1024):
             nc.vector.memset(windows[0][:, c0 : c0 + 512].bitcast(I32), 0)
-        for g, c0 in [(0, 1024), (0, 1536), (1, 0), (1, 512), (1, 1024), (1, 1536)]:
+        for g, c0 in [(0, 1536), (1, 0), (1, 512), (1, 1024), (1, 1536)]:
             nc.gpsimd.memset(windows[g][:, c0 : c0 + 512], 0.0)
         rw_ps = psum.tile([P, PACK, P], F32, name="rw_ps", tag="rw_ps")
         for c in range(PACK):
@@ -78,8 +81,6 @@ def tile_attend_depthffn_kernel(tc, tok_words, tok_scales, wa, wb, rw, res, offs
         rw_turned = psum.tile([P, I // CHUNK, P], F32, name="rw_turned", tag="rw_ps")
         for c in range(I // CHUNK):
             nc.tensor.transpose(rw_turned[:, c, :], rw_all[:, c * CHUNK : (c + 1) * CHUNK], ident[:])
-        rw_slot = held.tile([P, I // CHUNK], F32, name="rw_slot")
-        nc.scalar.copy(rw_slot[:], rw_turned[:, :, 0])
 
         tok_codes = held.tile([P, I], U16, name="tok_codes", align_bytes=64)
         tok_sc = held.tile([P, I], U8, name="tok_sc", align_bytes=64)
@@ -103,8 +104,14 @@ def tile_attend_depthffn_kernel(tc, tok_words, tok_scales, wa, wb, rw, res, offs
         nc.vector.tensor_copy(wb_bf[:], wb_raw.rearrange("p j e -> p e j"))
         nc.vector.quantize_mx(out=wb_codes[:].bitcast(FP8X4), scales=wb_sc[:], in_=wb_bf[:].rearrange("p e j -> p (e j)"))
 
-        res_low = held.tile([P, T], F32, name="res_low", tag="stage")
-        nc.sync.dma_start(res_low[:], res[:P, :])
+        rw_slot = shared.tile([P, I // CHUNK], F32, name="rw_slot", offset=4 * PACK * (F + E) - 32)
+        nc.scalar.copy(rw_slot[:], rw_turned[:, :, 0])
+
+        split = GPSIMD_CUTS[-1]
+        res_front = shared.tile([P, split], F32, name="res_front", offset=4 * (T - split))
+        nc.sync.dma_start(res_front[:], res[:P, :split])
+        res_back = shared.tile([P, T - split], F32, name="res_back", offset=0)
+        nc.sync.dma_start(res_back[:], res[:P, split:])
         res_high = held.tile([P, T], F32, name="res_high", tag="weights_bf", align_bytes=64)
         nc.sync.dma_start(res_high[:], res[P:, :])
 
@@ -149,24 +156,28 @@ def tile_attend_depthffn_kernel(tc, tok_words, tok_scales, wa, wb, rw, res, offs
 
         out_low = held.tile([P, GPSIMD_CUTS[-1]], F32, name="out_low")
         for c0, c1 in zip(GPSIMD_CUTS, GPSIMD_CUTS[1:]):
-            nc.gpsimd.tensor_tensor(out_low[:, c0:c1], res_low[:, c0:c1], windows[0][:, c0:c1], ADD)
+            nc.gpsimd.tensor_tensor(out_low[:, c0:c1], res_front[:, c0:c1], windows[0][:, c0:c1], ADD)
             nc.sync.dma_start(out[:P, c0:c1], out_low[:, c0:c1])
-        for u in range(3):
-            first = GPSIMD_CUTS[-1] + u * 2 * P
-            sum_ps = psum.tile([P, 2, P], F32, name="sum_ps%d" % u, tag="bank%d" % (2 * (u % 2) + 1))
-            for b in range(2):
-                tok = slice(first + b * P, first + (b + 1) * P)
-                nc.tensor.matmul(sum_ps[:, b, :], res_low[:, tok], ident[:], start=True, stop=False, is_transpose=True)
-                nc.tensor.matmul(sum_ps[:, b, :], windows[0][:, tok], ident[:], start=False, stop=True, is_transpose=True)
-            sum_turned = held.tile([P, 2, P], F32, name="sum_turned%d" % u)
-            nc.scalar.copy(sum_turned[:], sum_ps[:])
-            sum_back = psum.tile([P, 2, P], F32, name="sum_back%d" % u, tag="o_ps%d" % (u % 2))
-            for b in range(2):
-                nc.tensor.transpose(sum_back[:, b, :], sum_turned[:, b, :], ident[:])
-            sum_sb = held.tile([P, 2 * P], F32, name="sum_sb%d" % u)
+        sum_banks = ("bank0", "bank1", "bank2", "bank3", "o_ps0", "o_ps1")
+        back_banks = ("rw_ps", "bank7")
+        count = (T - split) // P
+        sums = [psum.tile([P, P], F32, name="sum_ps%d" % n, tag=sum_banks[n % len(sum_banks)]) for n in range(count)]
+        turned_sums = [held.tile([P, P], F32, name="sum_turned%d" % n) for n in range(count)]
+        for group in (range(len(sum_banks)), range(len(sum_banks), count)):
+            for n in group:
+                nc.tensor.matmul(sums[n][:], res_back[:, n * P : (n + 1) * P], ident[:], start=True, stop=False, is_transpose=True)
+            for n in group:
+                nc.tensor.matmul(sums[n][:], windows[0][:, split + n * P : split + (n + 1) * P], ident[:], start=False, stop=True, is_transpose=True)
+                nc.scalar.copy(turned_sums[n][:], sums[n][:])
+        for u, first in enumerate(range(0, count, 2)):
+            blocks = min(2, count - first)
+            sum_back = psum.tile([P, blocks, P], F32, name="sum_back%d" % u, tag=back_banks[u % 2])
+            for b in range(blocks):
+                nc.tensor.transpose(sum_back[:, b, :], turned_sums[first + b][:], ident[:])
+            sum_sb = held.tile([P, blocks * P], F32, name="sum_sb%d" % u)
             nc.scalar.copy(sum_sb[:], sum_back[:].rearrange("p b n -> p (b n)"))
-            nc.scalar.dma_start(out[:P, first : first + 2 * P], sum_sb[:])
-        out_high = held.tile([P, T], F32, name="out_high", tag="stage")
+            nc.scalar.dma_start(out[:P, split + first * P : split + (first + blocks) * P], sum_sb[:])
+        out_high = shared.tile([P, T], F32, name="out_high", offset=4 * (T - split))
         for c0, c1 in zip(STORE_CUTS, STORE_CUTS[1:]):
             nc.vector.tensor_tensor(out_high[:, c0:c1], res_high[:, c0:c1], windows[1][:, c0:c1], ADD)
             nc.sync.dma_start(out[P:, c0:c1], out_high[:, c0:c1])

@@ -23,6 +23,7 @@ PACK = 4
 CHUNK = 128
 HALF = 256
 WA_SPLIT = 88
+FILL = 64
 GPSIMD_CUTS = (0, 640, 1152)
 STORE_CUTS = (0, 256, 768, 1280, 1792, 2048)
 
@@ -98,11 +99,15 @@ def tile_attend_depthffn_kernel(tc, tok_words, tok_scales, wa, wb, rw, res, offs
             cols = slice(t * P, (t + 1) * P)
             nc.vector.quantize_mx(out=wa_codes[:, cols].bitcast(FP8X4), scales=wa_sc[:, cols], in_=wa_bf[:, t, :, :].rearrange("p m j -> p (m j)"))
 
-        wb_bf = held.tile([P, E, PACK], BF16, name="wb_bf", tag="weights_bf", align_bytes=64)
         wb_codes = held.tile([P, E], U32, name="wb_codes", align_bytes=64)
         wb_sc = held.tile([P, E], U8, name="wb_sc", align_bytes=64)
-        nc.vector.tensor_copy(wb_bf[:], wb_raw.rearrange("p j e -> p e j"))
-        nc.vector.quantize_mx(out=wb_codes[:].bitcast(FP8X4), scales=wb_sc[:], in_=wb_bf[:].rearrange("p e j -> p (e j)"))
+        wb_src = wb_raw.rearrange("p j e -> p e j")
+        wb_low = held.tile([P, P, PACK], BF16, name="wb_low", align_bytes=64)
+        nc.scalar.copy(wb_low[:], wb_src[:, :P])
+        nc.vector.quantize_mx(out=wb_codes[:, :P].bitcast(FP8X4), scales=wb_sc[:, :P], in_=wb_low[:].rearrange("p e j -> p (e j)"))
+        wb_high = held.tile([P, P, PACK], BF16, name="wb_high", tag="weights_bf", align_bytes=64)
+        nc.vector.tensor_copy(wb_high[:], wb_src[:, P:])
+        nc.vector.quantize_mx(out=wb_codes[:, P:].bitcast(FP8X4), scales=wb_sc[:, P:], in_=wb_high[:].rearrange("p e j -> p (e j)"))
 
         rw_slot = shared.tile([P, I // CHUNK], F32, name="rw_slot", offset=4 * PACK * (F + E) - 32)
         nc.scalar.copy(rw_slot[:], rw_turned[:, :, 0])
@@ -123,36 +128,38 @@ def tile_attend_depthffn_kernel(tc, tok_words, tok_scales, wa, wb, rw, res, offs
             for t in range(PACK):
                 cols = slice(t * P, (t + 1) * P)
                 mx_pass(nc, z_ps[:, t, :], wa_codes[:, cols].bitcast(FP8X4), wa_sc[:, cols], tok_codes[:, slots].bitcast(FP4X4), tok_sc[:, slots])
-            h_bf = held.tile([P, CHUNK, PACK], BF16, name="h_bf%d" % c, tag="h_bf%d" % (c if c < 3 else 1), align_bytes=64)
-            if c < 3:
+            h_bf = held.tile([P, CHUNK, PACK], BF16, name="h_bf%d" % c, align_bytes=64)
+            if c != 1:
                 nc.scalar.activation(h_bf[:], z_ps[:].rearrange("p t n -> p n t"), RELU)
             else:
                 nc.vector.tensor_scalar_max(h_bf[:], z_ps[:].rearrange("p t n -> p n t"), 0.0)
             nc.vector.quantize_mx(out=h_codes[:, slots].bitcast(FP8X4), scales=h_sc[:, slots], in_=h_bf[:].rearrange("p n t -> p (n t)"))
 
+        x_high = held.tile([P, I], F32, name="x_high")
+        nothing = held.tile([P, FILL], F32, name="nothing")
+        nc.vector.memset(nothing[:], 0.0)
         for h in range(2):
             slots = slice(h * HALF, (h + 1) * HALF)
             o_ps = psum.tile([P, HALF], F32, name="o_ps%d" % h, tag="o_ps%d" % h)
             mx_pass(nc, o_ps[:], wb_codes[:, :P].bitcast(FP8X4), wb_sc[:, :P], h_codes[:, slots].bitcast(FP8X4), h_sc[:, slots])
-            o_sb = held.tile([P, HALF], F32, name="o_sb%d" % h)
-            places = windows[0][:].indirect(offsets[:, h * HALF // 16 : (h + 1) * HALF // 16])
+            o_sb = held.tile([P, HALF], F32, name="o_sb%d" % h, tag="between%d" % h)
             nc.scalar.copy(o_sb[:], o_ps[:])
-            nc.vector.tensor_tensor(places, o_sb[:], rw_all[:, slots], MULT)
+            nc.vector.tensor_tensor(windows[0][:].indirect(offsets[:, h * HALF // 16 : (h + 1) * HALF // 16]), o_sb[:], rw_all[:, slots], MULT)
 
-        x_high = held.tile([P, I], F32, name="x_high")
-        for h in range(2):
             turned_ps = psum.tile([P, 2, P], F32, name="turned_ps%d" % h, tag="bank%d" % (2 * h))
-            turned = held.tile([P, 2, P], F32, name="turned%d" % h)
+            turned = held.tile([P, 2, P], F32, name="turned%d" % h, tag="between%d" % (h + 1))
             for u in range(2):
-                slots = slice((2 * h + u) * CHUNK, (2 * h + u + 1) * CHUNK)
-                mx_pass(nc, turned_ps[:, u, :], h_codes[:, slots].bitcast(FP8X4), h_sc[:, slots], wb_codes[:, P:].bitcast(FP8X4), wb_sc[:, P:])
+                chunk = slice((2 * h + u) * CHUNK, (2 * h + u + 1) * CHUNK)
+                mx_pass(nc, turned_ps[:, u, :], h_codes[:, chunk].bitcast(FP8X4), h_sc[:, chunk], wb_codes[:, P:].bitcast(FP8X4), wb_sc[:, P:])
             for u in range(2):
                 nc.scalar.activation(turned[:, u, :], turned_ps[:, u, :], COPY, scale=rw_slot[:, 2 * h + u : 2 * h + u + 1])
+            back_ps = psum.tile([P, 2, P], F32, name="back_ps%d" % h, tag="bank%d" % (2 * h + 1))
             for u in range(2):
-                back_ps = psum.tile([P, CHUNK], F32, name="back_ps%d%d" % (h, u), tag="bank%d" % (2 * u + 1))
-                nc.tensor.transpose(back_ps[:], turned[:, u, :], ident[:])
-                nc.scalar.copy(x_high[:, (2 * h + u) * CHUNK : (2 * h + u + 1) * CHUNK], back_ps[:])
-        nc.vector.tensor_copy(windows[1][:].indirect(offsets[:]), x_high[:])
+                nc.tensor.transpose(back_ps[:, u, :], turned[:, u, :], ident[:])
+            nc.scalar.copy(x_high[:, slots], back_ps[:].rearrange("p u n -> p (u n)"))
+            if h == 0:
+                nc.vector.tensor_tensor(windows[1][:].indirect(offsets[:, : FILL // 16]), x_high[:, :FILL], nothing[:], ADD)
+        nc.vector.tensor_copy(windows[1][:].indirect(offsets[:, FILL // 16 :]), x_high[:, FILL:])
 
         out_low = held.tile([P, GPSIMD_CUTS[-1]], F32, name="out_low")
         for c0, c1 in zip(GPSIMD_CUTS, GPSIMD_CUTS[1:]):

@@ -23,9 +23,9 @@ PACK = 4
 CHUNK = 128
 HALF = 256
 WA_SPLIT = 88
-FILL = 64
-GPSIMD_CUTS = (0, 640, 1152)
-STORE_CUTS = (0, 256, 768, 1280, 1792, 2048)
+LOW_CUTS = (0, 256, 768, 1408, 2048)
+EARLY = 256
+HIGH_CUTS = (0, 640, 1280, 1792, 2048)
 
 
 def mx_pass(nc, out, lhs_codes, lhs_scales, rhs_codes, rhs_scales):
@@ -79,14 +79,11 @@ def tile_attend_depthffn_kernel(tc, tok_words, tok_scales, wa, wb, rw, res, offs
             nc.tensor.transpose(rw_ps[:, c, :], rw_cols[:, c : c + 1].to_broadcast([P, P]), ident[:])
         rw_all = held.tile([P, I], F32, name="rw_all")
         nc.scalar.activation(rw_all[:].rearrange("p (n c) -> p n c", c=PACK), rw_ps[:].rearrange("p c n -> p n c"), COPY)
-        rw_turned = psum.tile([P, I // CHUNK, P], F32, name="rw_turned", tag="rw_ps")
-        for c in range(I // CHUNK):
-            nc.tensor.transpose(rw_turned[:, c, :], rw_all[:, c * CHUNK : (c + 1) * CHUNK], ident[:])
 
         tok_codes = held.tile([P, I], U16, name="tok_codes", align_bytes=64)
-        tok_sc = held.tile([P, I], U8, name="tok_sc", align_bytes=64)
+        tok_sc_first = held.tile([P, HALF], U8, name="tok_sc_first", align_bytes=64)
         nc.vector.tensor_copy(tok_codes[:], words[:].indirect(offsets[:]))
-        nc.vector.tensor_copy(tok_sc[:], scale_rows[:].indirect(offsets[:]))
+        nc.vector.tensor_copy(tok_sc_first[:], scale_rows[:].indirect(offsets[:, : HALF // 16]))
 
         wa_bf = held.tile([P, PACK, P, PACK], BF16, name="wa_bf", tag="weights_bf", align_bytes=64)
         wa_dst = wa_bf[:].rearrange("p t m j -> p m t j")
@@ -99,92 +96,63 @@ def tile_attend_depthffn_kernel(tc, tok_words, tok_scales, wa, wb, rw, res, offs
             cols = slice(t * P, (t + 1) * P)
             nc.vector.quantize_mx(out=wa_codes[:, cols].bitcast(FP8X4), scales=wa_sc[:, cols], in_=wa_bf[:, t, :, :].rearrange("p m j -> p (m j)"))
 
+        tok_sc_second = held.tile([P, HALF], U8, name="tok_sc_second", tag="weights_bf", align_bytes=64)
+        nc.vector.tensor_copy(tok_sc_second[:], scale_rows[:].indirect(offsets[:, HALF // 16 :]))
+        tok_sc = (tok_sc_first, tok_sc_second)
+
         wb_codes = held.tile([P, E], U32, name="wb_codes", align_bytes=64)
         wb_sc = held.tile([P, E], U8, name="wb_sc", align_bytes=64)
         wb_src = wb_raw.rearrange("p j e -> p e j")
         wb_low = held.tile([P, P, PACK], BF16, name="wb_low", align_bytes=64)
         nc.scalar.copy(wb_low[:], wb_src[:, :P])
         nc.vector.quantize_mx(out=wb_codes[:, :P].bitcast(FP8X4), scales=wb_sc[:, :P], in_=wb_low[:].rearrange("p e j -> p (e j)"))
-        wb_high = held.tile([P, P, PACK], BF16, name="wb_high", tag="weights_bf", align_bytes=64)
-        nc.vector.tensor_copy(wb_high[:], wb_src[:, P:])
+        wb_high = held.tile([P, P, PACK], BF16, name="wb_high", align_bytes=64)
+        nc.scalar.copy(wb_high[:], wb_src[:, P:])
         nc.vector.quantize_mx(out=wb_codes[:, P:].bitcast(FP8X4), scales=wb_sc[:, P:], in_=wb_high[:].rearrange("p e j -> p (e j)"))
 
-        rw_slot = shared.tile([P, I // CHUNK], F32, name="rw_slot", offset=4 * PACK * (F + E) - 32)
-        nc.scalar.copy(rw_slot[:], rw_turned[:, :, 0])
-
-        split = GPSIMD_CUTS[-1]
-        res_front = shared.tile([P, split], F32, name="res_front", offset=4 * (T - split))
-        nc.sync.dma_start(res_front[:], res[:P, :split])
-        res_back = shared.tile([P, T - split], F32, name="res_back", offset=0)
-        nc.sync.dma_start(res_back[:], res[:P, split:])
+        res_low = shared.tile([P, T], F32, name="res_low", offset=0)
+        nc.sync.dma_start(res_low[:], res[:P, :])
         res_high = held.tile([P, T], F32, name="res_high", tag="weights_bf", align_bytes=64)
         nc.sync.dma_start(res_high[:], res[P:, :])
 
         h_codes = held.tile([P, I], U32, name="h_codes", align_bytes=64)
         h_sc = held.tile([P, I], U8, name="h_sc", align_bytes=64)
-        for c in range(I // CHUNK):
-            slots = slice(c * CHUNK, (c + 1) * CHUNK)
-            z_ps = psum.tile([P, PACK, CHUNK], F32, name="z_ps%d" % c, tag="bank%d" % c)
-            for t in range(PACK):
-                cols = slice(t * P, (t + 1) * P)
-                mx_pass(nc, z_ps[:, t, :], wa_codes[:, cols].bitcast(FP8X4), wa_sc[:, cols], tok_codes[:, slots].bitcast(FP4X4), tok_sc[:, slots])
-            h_bf = held.tile([P, CHUNK, PACK], BF16, name="h_bf%d" % c, align_bytes=64)
-            if c != 1:
-                nc.scalar.activation(h_bf[:], z_ps[:].rearrange("p t n -> p n t"), RELU)
-            else:
-                nc.vector.tensor_scalar_max(h_bf[:], z_ps[:].rearrange("p t n -> p n t"), 0.0)
-            nc.vector.quantize_mx(out=h_codes[:, slots].bitcast(FP8X4), scales=h_sc[:, slots], in_=h_bf[:].rearrange("p n t -> p (n t)"))
-
-        x_high = held.tile([P, I], F32, name="x_high")
-        nothing = held.tile([P, FILL], F32, name="nothing")
-        nc.vector.memset(nothing[:], 0.0)
+        high_ps = psum.tile([P, I], F32, name="high_ps", tag="high_ps")
         for h in range(2):
+            for c in (2 * h, 2 * h + 1):
+                chunk = slice(c * CHUNK, (c + 1) * CHUNK)
+                z_ps = psum.tile([P, PACK, CHUNK], F32, name="z_ps%d" % c, tag="bank%d" % c)
+                for t in range(PACK):
+                    cols = slice(t * P, (t + 1) * P)
+                    mx_pass(nc, z_ps[:, t, :], wa_codes[:, cols].bitcast(FP8X4), wa_sc[:, cols], tok_codes[:, chunk].bitcast(FP4X4), tok_sc[h][:, (c % 2) * CHUNK : (c % 2 + 1) * CHUNK])
+                h_bf = shared.tile([P, CHUNK, PACK], BF16, name="h_bf%d" % c, align_bytes=64, offset=4 * PACK * F + 2 * PACK * CHUNK * c)
+                if c != 1:
+                    nc.scalar.activation(h_bf[:], z_ps[:].rearrange("p t n -> p n t"), RELU)
+                else:
+                    nc.vector.tensor_scalar_max(h_bf[:], z_ps[:].rearrange("p t n -> p n t"), 0.0)
+                nc.vector.quantize_mx(out=h_codes[:, chunk].bitcast(FP8X4), scales=h_sc[:, chunk], in_=h_bf[:].rearrange("p n t -> p (n t)"))
             slots = slice(h * HALF, (h + 1) * HALF)
-            o_ps = psum.tile([P, HALF], F32, name="o_ps%d" % h, tag="o_ps%d" % h)
-            mx_pass(nc, o_ps[:], wb_codes[:, :P].bitcast(FP8X4), wb_sc[:, :P], h_codes[:, slots].bitcast(FP8X4), h_sc[:, slots])
-            o_sb = held.tile([P, HALF], F32, name="o_sb%d" % h, tag="between%d" % h)
-            nc.scalar.copy(o_sb[:], o_ps[:])
-            nc.vector.tensor_tensor(windows[0][:].indirect(offsets[:, h * HALF // 16 : (h + 1) * HALF // 16]), o_sb[:], rw_all[:, slots], MULT)
+            low_ps = psum.tile([P, HALF], F32, name="low_ps%d" % h, tag="low_ps%d" % h)
+            mx_pass(nc, low_ps[:], wb_codes[:, :P].bitcast(FP8X4), wb_sc[:, :P], h_codes[:, slots].bitcast(FP8X4), h_sc[:, slots])
+            x_low = held.tile([P, HALF], F32, name="x_low%d" % h)
+            nc.vector.tensor_tensor(x_low[:], low_ps[:], rw_all[:, slots], MULT)
+            nc.scalar.activation(windows[0][:].indirect(offsets[:, h * HALF // 16 : (h + 1) * HALF // 16]), x_low[:], COPY)
+            mx_pass(nc, high_ps[:, slots], wb_codes[:, P:].bitcast(FP8X4), wb_sc[:, P:], h_codes[:, slots].bitcast(FP8X4), h_sc[:, slots])
 
-            turned_ps = psum.tile([P, 2, P], F32, name="turned_ps%d" % h, tag="bank%d" % (2 * h))
-            turned = held.tile([P, 2, P], F32, name="turned%d" % h, tag="between%d" % (h + 1))
-            for u in range(2):
-                chunk = slice((2 * h + u) * CHUNK, (2 * h + u + 1) * CHUNK)
-                mx_pass(nc, turned_ps[:, u, :], h_codes[:, chunk].bitcast(FP8X4), h_sc[:, chunk], wb_codes[:, P:].bitcast(FP8X4), wb_sc[:, P:])
-            for u in range(2):
-                nc.scalar.activation(turned[:, u, :], turned_ps[:, u, :], COPY, scale=rw_slot[:, 2 * h + u : 2 * h + u + 1])
-            back_ps = psum.tile([P, 2, P], F32, name="back_ps%d" % h, tag="bank%d" % (2 * h + 1))
-            for u in range(2):
-                nc.tensor.transpose(back_ps[:, u, :], turned[:, u, :], ident[:])
-            nc.scalar.copy(x_high[:, slots], back_ps[:].rearrange("p u n -> p (u n)"))
-            if h == 0:
-                nc.vector.tensor_tensor(windows[1][:].indirect(offsets[:, : FILL // 16]), x_high[:, :FILL], nothing[:], ADD)
-        nc.vector.tensor_copy(windows[1][:].indirect(offsets[:, FILL // 16 :]), x_high[:, FILL:])
+        nothing = held.tile([P, EARLY], F32, name="nothing")
+        nc.vector.memset(nothing[:], 0.0)
+        x_early = held.tile([P, EARLY], F32, name="x_early")
+        nc.vector.tensor_tensor(x_early[:], high_ps[:, :EARLY], rw_all[:, :EARLY], MULT)
+        x_late = held.tile([P, I - EARLY], F32, name="x_late")
+        nc.vector.tensor_tensor(x_late[:], high_ps[:, EARLY:], rw_all[:, EARLY:], MULT)
+        nc.vector.tensor_tensor(windows[1][:].indirect(offsets[:, : EARLY // 16]), x_early[:], nothing[:], ADD)
+        nc.scalar.activation(windows[1][:].indirect(offsets[:, EARLY // 16 :]), x_late[:], COPY)
 
-        out_low = held.tile([P, GPSIMD_CUTS[-1]], F32, name="out_low")
-        for c0, c1 in zip(GPSIMD_CUTS, GPSIMD_CUTS[1:]):
-            nc.gpsimd.tensor_tensor(out_low[:, c0:c1], res_front[:, c0:c1], windows[0][:, c0:c1], ADD)
+        out_low = held.tile([P, T], F32, name="out_low")
+        for c0, c1 in zip(LOW_CUTS, LOW_CUTS[1:]):
+            nc.vector.tensor_tensor(out_low[:, c0:c1], res_low[:, c0:c1], windows[0][:, c0:c1], ADD)
             nc.sync.dma_start(out[:P, c0:c1], out_low[:, c0:c1])
-        sum_banks = ("bank0", "bank1", "bank2", "bank3", "o_ps0", "o_ps1")
-        back_banks = ("rw_ps", "bank7")
-        count = (T - split) // P
-        sums = [psum.tile([P, P], F32, name="sum_ps%d" % n, tag=sum_banks[n % len(sum_banks)]) for n in range(count)]
-        turned_sums = [held.tile([P, P], F32, name="sum_turned%d" % n) for n in range(count)]
-        for group in (range(len(sum_banks)), range(len(sum_banks), count)):
-            for n in group:
-                nc.tensor.matmul(sums[n][:], res_back[:, n * P : (n + 1) * P], ident[:], start=True, stop=False, is_transpose=True)
-            for n in group:
-                nc.tensor.matmul(sums[n][:], windows[0][:, split + n * P : split + (n + 1) * P], ident[:], start=False, stop=True, is_transpose=True)
-                nc.scalar.copy(turned_sums[n][:], sums[n][:])
-        for u, first in enumerate(range(0, count, 2)):
-            blocks = min(2, count - first)
-            sum_back = psum.tile([P, blocks, P], F32, name="sum_back%d" % u, tag=back_banks[u % 2])
-            for b in range(blocks):
-                nc.tensor.transpose(sum_back[:, b, :], turned_sums[first + b][:], ident[:])
-            sum_sb = held.tile([P, blocks * P], F32, name="sum_sb%d" % u)
-            nc.scalar.copy(sum_sb[:], sum_back[:].rearrange("p b n -> p (b n)"))
-            nc.scalar.dma_start(out[:P, split + first * P : split + (first + blocks) * P], sum_sb[:])
-        out_high = shared.tile([P, T], F32, name="out_high", offset=4 * (T - split))
-        for c0, c1 in zip(STORE_CUTS, STORE_CUTS[1:]):
+        out_high = held.tile([P, T], F32, name="out_high")
+        for c0, c1 in zip(HIGH_CUTS, HIGH_CUTS[1:]):
             nc.vector.tensor_tensor(out_high[:, c0:c1], res_high[:, c0:c1], windows[1][:, c0:c1], ADD)
             nc.sync.dma_start(out[P:, c0:c1], out_high[:, c0:c1])

@@ -23,9 +23,11 @@ PACK = 4
 CHUNK = 128
 HALF = 256
 WA_SPLIT = 88
+VECTOR_ZERO_CUTS = (0, 703, 1408)
+GPSIMD_ZERO_PIECES = ((0, 1408, 2048), (1, 0, 768), (1, 768, 1408), (1, 1408, 1792), (1, 1792, 2048))
 LOW_CUTS = (0, 256, 768, 1408, 2048)
-EARLY = 256
 HIGH_CUTS = (0, 640, 1280, 1792, 2048)
+LOW_AT, WA_AT, WB_AT, WORDS_AT, ROUNDED_AT, SCALES_AT = 0, 6144, 14336, 18432, 26624, 30720
 
 
 def mx_pass(nc, out, lhs_codes, lhs_scales, rhs_codes, rhs_scales):
@@ -40,96 +42,90 @@ def tile_attend_depthffn_kernel(tc, tok_words, tok_scales, wa, wb, rw, res, offs
         psum = ctx.enter_context(tc.psum_pool(name="psum", bufs=1))
 
         offsets = held.tile([P, I // 16], U16, name="offsets")
-        words = held.tile([P, T], U16, name="words", align_bytes=64)
-        nc.sync.dma_start(words[:].bitcast(I32), tok_words[0].bitcast(I32))
-        nc.sync.dma_start(offsets[:], offs)
-
-        rw_cols = held.tile([P, PACK], F32, name="rw_cols")
-        nc.scalar.dma_start(rw_cols[:], rw.rearrange("o (p c) -> (o p) c", c=PACK))
-
-        scale_rows = held.tile([P, T], U8, name="scale_rows", align_bytes=64)
-        nc.gpsimd.memset(scale_rows[:].bitcast(I32), 0)
-        scales_by_r = tok_scales[0].bitcast(I32).rearrange("(q r) c -> r q c", r=4)
-        for r in range(4):
-            queue = nc.sync if r < 2 else nc.scalar
-            queue.dma_start(scale_rows[r:P:32, :].bitcast(I32), scales_by_r[r])
-
-
-        zeros = shared.tile([P, P], F32, name="zeros", offset=0)
+        scale_rows = shared.tile([P, T], U8, name="scale_rows", align_bytes=64, offset=SCALES_AT)
+        nc.vector.memset(scale_rows[:].bitcast(I32), 0)
+        zeros = held.tile([P, P], F32, name="zeros")
         nc.vector.memset(zeros[:], 0.0)
+
+        wa_raw = shared.tile([P, PACK * F], F32, name="wa_raw", align_bytes=64, offset=WA_AT)
+        wa_rows = wa.rearrange("(p j) f -> p (j f)", j=PACK)
+        nc.sync.dma_start(offsets[:], offs)
+        nc.sync.dma_start(wa_raw[:, : 2 * F], wa_rows[:, : 2 * F])
+        scales_by_r = tok_scales[0].bitcast(I32).rearrange("(q r) c -> r q c", r=4)
+        for r in range(2):
+            nc.sync.dma_start(scale_rows[r:P:32, :].bitcast(I32), scales_by_r[r])
+        nc.sync.dma_start(wa_raw[:, 2 * F :], wa_rows[:, 2 * F :])
+        words = shared.tile([P, T], U16, name="words", align_bytes=64, offset=WORDS_AT)
+        nc.sync.dma_start(words[:].bitcast(I32), tok_words[0].bitcast(I32))
+
+        rw_cols = shared.tile([P, PACK], F32, name="rw_cols", align_bytes=64, offset=ROUNDED_AT)
+        nc.scalar.dma_start(rw_cols[:], rw.rearrange("o (p c) -> (o p) c", c=PACK))
+        for r in range(2, 4):
+            nc.scalar.dma_start(scale_rows[r:P:32, :].bitcast(I32), scales_by_r[r])
+        wb_raw = shared.tile([P, PACK * E], F32, name="wb_raw", align_bytes=64, offset=WB_AT)
+        nc.sync.dma_start(wb_raw[:], wb.rearrange("(p j) e -> p (j e)", j=PACK))
+
         ident = held.tile([P, P], F32, name="ident")
         nc.gpsimd.affine_select(out=ident[:], in_=zeros[:], compare_op=mybir.AluOpType.not_equal, fill=1.0, base=0, pattern=[[-1, P]], channel_multiplier=1)
-
-        w_raw = shared.tile([P, PACK * (F + E)], F32, name="w_raw", offset=0)
-        wa_raw = w_raw[:, : PACK * F].rearrange("p (j f) -> p j f", j=PACK)
-        wb_raw = w_raw[:, PACK * F :].rearrange("p (j e) -> p j e", j=PACK)
-        nc.sync.dma_start(wa_raw, wa.rearrange("(p j) f -> p j f", j=PACK))
-        nc.sync.dma_start(wb_raw, wb.rearrange("(p j) e -> p j e", j=PACK))
 
         windows = []
         for g in range(2):
             w = held.tile([P, T], F32, name="window%d" % g)
             windows.append(w)
-        for c0 in (0, 512, 1024):
-            nc.vector.memset(windows[0][:, c0 : c0 + 512].bitcast(I32), 0)
-        for g, c0 in [(0, 1536), (1, 0), (1, 512), (1, 1024), (1, 1536)]:
-            nc.gpsimd.memset(windows[g][:, c0 : c0 + 512], 0.0)
+        for c0, c1 in zip(VECTOR_ZERO_CUTS, VECTOR_ZERO_CUTS[1:]):
+            nc.vector.memset(windows[0][:, c0:c1], 0.0)
+        for g, c0, c1 in GPSIMD_ZERO_PIECES:
+            nc.gpsimd.memset(windows[g][:, c0:c1], 0.0)
+
         rw_ps = psum.tile([P, PACK, P], F32, name="rw_ps", tag="rw_ps")
         for c in range(PACK):
             nc.tensor.transpose(rw_ps[:, c, :], rw_cols[:, c : c + 1].to_broadcast([P, P]), ident[:])
         rw_all = held.tile([P, I], F32, name="rw_all")
         nc.scalar.activation(rw_all[:].rearrange("p (n c) -> p n c", c=PACK), rw_ps[:].rearrange("p c n -> p n c"), COPY)
 
-        tok_codes = held.tile([P, I], U16, name="tok_codes", align_bytes=64)
-        tok_sc_first = held.tile([P, HALF], U8, name="tok_sc_first", align_bytes=64)
-        nc.vector.tensor_copy(tok_codes[:], words[:].indirect(offsets[:]))
-        nc.vector.tensor_copy(tok_sc_first[:], scale_rows[:].indirect(offsets[:, : HALF // 16]))
+        tok_sc = held.tile([P, I], U8, name="tok_sc", align_bytes=64)
+        nc.vector.tensor_copy(tok_sc[:], scale_rows[:].indirect(offsets[:]))
 
-        wa_bf = held.tile([P, PACK, P, PACK], BF16, name="wa_bf", tag="weights_bf", align_bytes=64)
+        wa_bf = shared.tile([P, PACK, P, PACK], BF16, name="wa_bf", align_bytes=64, offset=ROUNDED_AT)
         wa_dst = wa_bf[:].rearrange("p t m j -> p m t j")
-        wa_src = wa_raw.rearrange("p j (m t) -> p m t j", t=PACK)
+        wa_src = wa_raw[:].rearrange("p (j m t) -> p m t j", j=PACK, t=PACK)
         nc.vector.tensor_copy(wa_dst[:, :WA_SPLIT], wa_src[:, :WA_SPLIT])
         nc.scalar.copy(wa_dst[:, WA_SPLIT:], wa_src[:, WA_SPLIT:])
+        tok_first = shared.tile([P, HALF], U16, name="tok_first", align_bytes=64, offset=WA_AT + 6144)
+        nc.vector.tensor_copy(tok_first[:], words[:].indirect(offsets[:, : HALF // 16]))
         wa_codes = held.tile([P, F], U32, name="wa_codes", align_bytes=64)
         wa_sc = held.tile([P, F], U8, name="wa_sc", align_bytes=64)
         for t in range(PACK):
             cols = slice(t * P, (t + 1) * P)
             nc.vector.quantize_mx(out=wa_codes[:, cols].bitcast(FP8X4), scales=wa_sc[:, cols], in_=wa_bf[:, t, :, :].rearrange("p m j -> p (m j)"))
+        tok_second = shared.tile([P, HALF], U16, name="tok_second", align_bytes=64, offset=ROUNDED_AT)
+        nc.vector.tensor_copy(tok_second[:], words[:].indirect(offsets[:, HALF // 16 :]))
+        tok_codes = (tok_first, tok_second)
 
-        tok_sc_second = held.tile([P, HALF], U8, name="tok_sc_second", tag="weights_bf", align_bytes=64)
-        nc.vector.tensor_copy(tok_sc_second[:], scale_rows[:].indirect(offsets[:, HALF // 16 :]))
-        tok_sc = (tok_sc_first, tok_sc_second)
-
+        wb_src = wb_raw[:].rearrange("p (j c i) -> p c j i", j=PACK, i=4)
+        wb_bf = shared.tile([P, E, PACK], BF16, name="wb_bf", align_bytes=64, offset=ROUNDED_AT + 2048)
+        nc.vector.tensor_copy(wb_bf[:].rearrange("p (c i) j -> p c j i", i=4), wb_src)
         wb_codes = held.tile([P, E], U32, name="wb_codes", align_bytes=64)
         wb_sc = held.tile([P, E], U8, name="wb_sc", align_bytes=64)
-        wb_src = wb_raw.rearrange("p j e -> p e j")
-        wb_low = held.tile([P, P, PACK], BF16, name="wb_low", align_bytes=64)
-        nc.scalar.copy(wb_low[:], wb_src[:, :P])
-        nc.vector.quantize_mx(out=wb_codes[:, :P].bitcast(FP8X4), scales=wb_sc[:, :P], in_=wb_low[:].rearrange("p e j -> p (e j)"))
-        wb_high = held.tile([P, P, PACK], BF16, name="wb_high", align_bytes=64)
-        nc.scalar.copy(wb_high[:], wb_src[:, P:])
-        nc.vector.quantize_mx(out=wb_codes[:, P:].bitcast(FP8X4), scales=wb_sc[:, P:], in_=wb_high[:].rearrange("p e j -> p (e j)"))
+        nc.vector.quantize_mx(out=wb_codes[:, :P].bitcast(FP8X4), scales=wb_sc[:, :P], in_=wb_bf[:, :P].rearrange("p e j -> p (e j)"))
 
-        res_low = shared.tile([P, T], F32, name="res_low", offset=0)
+        res_low = shared.tile([P, T], F32, name="res_low", align_bytes=64, offset=LOW_AT)
         nc.sync.dma_start(res_low[:], res[:P, :])
-        res_high = held.tile([P, T], F32, name="res_high", tag="weights_bf", align_bytes=64)
+        res_high = shared.tile([P, T], F32, name="res_high", align_bytes=64, offset=WORDS_AT)
         nc.sync.dma_start(res_high[:], res[P:, :])
 
-        h_codes = held.tile([P, I], U32, name="h_codes", align_bytes=64)
+        h_codes = shared.tile([P, I], U32, name="h_codes", align_bytes=64, offset=WB_AT)
         h_sc = held.tile([P, I], U8, name="h_sc", align_bytes=64)
         high_ps = psum.tile([P, I], F32, name="high_ps", tag="high_ps")
         for h in range(2):
             for c in (2 * h, 2 * h + 1):
                 chunk = slice(c * CHUNK, (c + 1) * CHUNK)
                 z_ps = psum.tile([P, PACK, CHUNK], F32, name="z_ps%d" % c, tag="bank%d" % c)
-                for t in range(PACK):
+                for t in (range(PACK) if c % 2 == 0 else reversed(range(PACK))):
                     cols = slice(t * P, (t + 1) * P)
-                    mx_pass(nc, z_ps[:, t, :], wa_codes[:, cols].bitcast(FP8X4), wa_sc[:, cols], tok_codes[:, chunk].bitcast(FP4X4), tok_sc[h][:, (c % 2) * CHUNK : (c % 2 + 1) * CHUNK])
-                h_bf = shared.tile([P, CHUNK, PACK], BF16, name="h_bf%d" % c, align_bytes=64, offset=4 * PACK * F + 2 * PACK * CHUNK * c)
-                if c != 1:
-                    nc.scalar.activation(h_bf[:], z_ps[:].rearrange("p t n -> p n t"), RELU)
-                else:
-                    nc.vector.tensor_scalar_max(h_bf[:], z_ps[:].rearrange("p t n -> p n t"), 0.0)
+                    mx_pass(nc, z_ps[:, t, :], wa_codes[:, cols].bitcast(FP8X4), wa_sc[:, cols], tok_codes[h][:, (c % 2) * CHUNK : (c % 2 + 1) * CHUNK].bitcast(FP4X4), tok_sc[:, chunk])
+                h_bf = held.tile([P, CHUNK, PACK], BF16, name="h_bf%d" % c, align_bytes=64)
+                nc.scalar.activation(h_bf[:], z_ps[:].rearrange("p t n -> p n t"), RELU)
                 nc.vector.quantize_mx(out=h_codes[:, chunk].bitcast(FP8X4), scales=h_sc[:, chunk], in_=h_bf[:].rearrange("p n t -> p (n t)"))
             slots = slice(h * HALF, (h + 1) * HALF)
             low_ps = psum.tile([P, HALF], F32, name="low_ps%d" % h, tag="low_ps%d" % h)
@@ -137,16 +133,16 @@ def tile_attend_depthffn_kernel(tc, tok_words, tok_scales, wa, wb, rw, res, offs
             x_low = held.tile([P, HALF], F32, name="x_low%d" % h)
             nc.vector.tensor_tensor(x_low[:], low_ps[:], rw_all[:, slots], MULT)
             nc.scalar.activation(windows[0][:].indirect(offsets[:, h * HALF // 16 : (h + 1) * HALF // 16]), x_low[:], COPY)
+            if h == 0:
+                nc.vector.quantize_mx(out=wb_codes[:, P:].bitcast(FP8X4), scales=wb_sc[:, P:], in_=wb_bf[:, P:].rearrange("p e j -> p (e j)"))
             mx_pass(nc, high_ps[:, slots], wb_codes[:, P:].bitcast(FP8X4), wb_sc[:, P:], h_codes[:, slots].bitcast(FP8X4), h_sc[:, slots])
 
-        nothing = held.tile([P, EARLY], F32, name="nothing")
-        nc.vector.memset(nothing[:], 0.0)
-        x_early = held.tile([P, EARLY], F32, name="x_early")
-        nc.vector.tensor_tensor(x_early[:], high_ps[:, :EARLY], rw_all[:, :EARLY], MULT)
-        x_late = held.tile([P, I - EARLY], F32, name="x_late")
-        nc.vector.tensor_tensor(x_late[:], high_ps[:, EARLY:], rw_all[:, EARLY:], MULT)
-        nc.vector.tensor_tensor(windows[1][:].indirect(offsets[:, : EARLY // 16]), x_early[:], nothing[:], ADD)
-        nc.scalar.activation(windows[1][:].indirect(offsets[:, EARLY // 16 :]), x_late[:], COPY)
+        x_early = held.tile([P, HALF], F32, name="x_early")
+        nc.vector.tensor_tensor(x_early[:], high_ps[:, :HALF], rw_all[:, :HALF], MULT)
+        x_late = held.tile([P, HALF], F32, name="x_late")
+        nc.vector.tensor_tensor(x_late[:], high_ps[:, HALF:], rw_all[:, HALF:], MULT)
+        nc.vector.tensor_copy(windows[1][:].indirect(offsets[:, : HALF // 16]), x_early[:])
+        nc.scalar.activation(windows[1][:].indirect(offsets[:, HALF // 16 :]), x_late[:], COPY)
 
         out_low = held.tile([P, T], F32, name="out_low")
         for c0, c1 in zip(LOW_CUTS, LOW_CUTS[1:]):

@@ -52,7 +52,7 @@ def tile_attend_depthffn_kernel(tc, tok_words, tok_scales, wa, wb, rw, res, offs
         nc.sync.dma_start(offsets[:], offs)
         nc.sync.dma_start(wa_raw[:, : 2 * F], wa_rows[:, : 2 * F])
         scales_by_r = tok_scales[0].bitcast(I32).rearrange("(q r) c -> r q c", r=4)
-        for r in range(2):
+        for r in range(4):
             nc.sync.dma_start(scale_rows[r:P:32, :].bitcast(I32), scales_by_r[r])
         nc.sync.dma_start(wa_raw[:, 2 * F :], wa_rows[:, 2 * F :])
         words = shared.tile([P, T], U16, name="words", align_bytes=64, offset=WORDS_AT)
@@ -60,8 +60,6 @@ def tile_attend_depthffn_kernel(tc, tok_words, tok_scales, wa, wb, rw, res, offs
 
         rw_cols = shared.tile([P, PACK], F32, name="rw_cols", align_bytes=64, offset=ROUNDED_AT)
         nc.scalar.dma_start(rw_cols[:], rw.rearrange("o (p c) -> (o p) c", c=PACK))
-        for r in range(2, 4):
-            nc.scalar.dma_start(scale_rows[r:P:32, :].bitcast(I32), scales_by_r[r])
         wb_raw = shared.tile([P, PACK * E], F32, name="wb_raw", align_bytes=64, offset=WB_AT)
         nc.sync.dma_start(wb_raw[:], wb.rearrange("(p j) e -> p (j e)", j=PACK))
 

@@ -23,6 +23,7 @@ PACK = 4
 CHUNK = 128
 HALF = 256
 WA_SPLIT = 88
+HIGH_SPLIT = 320
 VECTOR_ZERO_CUTS = (0, 703, 1408)
 GPSIMD_ZERO_PIECES = ((0, 1408, 2048), (1, 0, 768), (1, 768, 1408), (1, 1408, 1792), (1, 1792, 2048))
 LOW_CUTS = (0, 256, 768, 1408, 2048)
@@ -72,6 +73,8 @@ def tile_attend_depthffn_kernel(tc, tok_words, tok_scales, wa, wb, rw, res, offs
             windows.append(w)
         for c0, c1 in zip(VECTOR_ZERO_CUTS, VECTOR_ZERO_CUTS[1:]):
             nc.vector.memset(windows[0][:, c0:c1], 0.0)
+        nothing = held.tile([P, I - HIGH_SPLIT], F32, name="nothing")
+        nc.vector.memset(nothing[:], 0.0)
         for g, c0, c1 in GPSIMD_ZERO_PIECES:
             nc.gpsimd.memset(windows[g][:, c0:c1], 0.0)
 
@@ -96,12 +99,12 @@ def tile_attend_depthffn_kernel(tc, tok_words, tok_scales, wa, wb, rw, res, offs
         for t in range(PACK):
             cols = slice(t * P, (t + 1) * P)
             nc.vector.quantize_mx(out=wa_codes[:, cols].bitcast(FP8X4), scales=wa_sc[:, cols], in_=wa_bf[:, t, :, :].rearrange("p m j -> p (m j)"))
-        tok_second = shared.tile([P, HALF], U16, name="tok_second", align_bytes=64, offset=ROUNDED_AT)
+        tok_second = shared.tile([P, HALF], U16, name="tok_second", align_bytes=64, offset=WA_AT + 6656)
         nc.vector.tensor_copy(tok_second[:], words[:].indirect(offsets[:, HALF // 16 :]))
         tok_codes = (tok_first, tok_second)
 
         wb_src = wb_raw[:].rearrange("p (j c i) -> p c j i", j=PACK, i=4)
-        wb_bf = shared.tile([P, E, PACK], BF16, name="wb_bf", align_bytes=64, offset=ROUNDED_AT + 2048)
+        wb_bf = shared.tile([P, E, PACK], BF16, name="wb_bf", align_bytes=64, offset=WA_AT + 4096)
         nc.vector.tensor_copy(wb_bf[:].rearrange("p (c i) j -> p c j i", i=4), wb_src)
         wb_codes = held.tile([P, E], U32, name="wb_codes", align_bytes=64)
         wb_sc = held.tile([P, E], U8, name="wb_sc", align_bytes=64)
@@ -112,35 +115,54 @@ def tile_attend_depthffn_kernel(tc, tok_words, tok_scales, wa, wb, rw, res, offs
         res_high = shared.tile([P, T], F32, name="res_high", align_bytes=64, offset=WORDS_AT)
         nc.sync.dma_start(res_high[:], res[P:, :])
 
-        h_codes = shared.tile([P, I], U32, name="h_codes", align_bytes=64, offset=WB_AT)
-        h_sc = held.tile([P, I], U8, name="h_sc", align_bytes=64)
-        high_ps = psum.tile([P, I], F32, name="high_ps", tag="high_ps")
-        for h in range(2):
-            for c in (2 * h, 2 * h + 1):
-                chunk = slice(c * CHUNK, (c + 1) * CHUNK)
-                z_ps = psum.tile([P, PACK, CHUNK], F32, name="z_ps%d" % c, tag="bank%d" % c)
-                for t in (range(PACK) if c % 2 == 0 else reversed(range(PACK))):
-                    cols = slice(t * P, (t + 1) * P)
-                    mx_pass(nc, z_ps[:, t, :], wa_codes[:, cols].bitcast(FP8X4), wa_sc[:, cols], tok_codes[h][:, (c % 2) * CHUNK : (c % 2 + 1) * CHUNK].bitcast(FP4X4), tok_sc[:, chunk])
-                h_bf = held.tile([P, CHUNK, PACK], BF16, name="h_bf%d" % c, align_bytes=64)
-                nc.scalar.activation(h_bf[:], z_ps[:].rearrange("p t n -> p n t"), RELU)
-                nc.vector.quantize_mx(out=h_codes[:, chunk].bitcast(FP8X4), scales=h_sc[:, chunk], in_=h_bf[:].rearrange("p n t -> p (n t)"))
-            slots = slice(h * HALF, (h + 1) * HALF)
-            low_ps = psum.tile([P, HALF], F32, name="low_ps%d" % h, tag="low_ps%d" % h)
-            mx_pass(nc, low_ps[:], wb_codes[:, :P].bitcast(FP8X4), wb_sc[:, :P], h_codes[:, slots].bitcast(FP8X4), h_sc[:, slots])
-            x_low = held.tile([P, HALF], F32, name="x_low%d" % h)
-            nc.vector.tensor_tensor(x_low[:], low_ps[:], rw_all[:, slots], MULT)
-            nc.scalar.activation(windows[0][:].indirect(offsets[:, h * HALF // 16 : (h + 1) * HALF // 16]), x_low[:], COPY)
-            if h == 0:
-                nc.vector.quantize_mx(out=wb_codes[:, P:].bitcast(FP8X4), scales=wb_sc[:, P:], in_=wb_bf[:, P:].rearrange("p e j -> p (e j)"))
-            mx_pass(nc, high_ps[:, slots], wb_codes[:, P:].bitcast(FP8X4), wb_sc[:, P:], h_codes[:, slots].bitcast(FP8X4), h_sc[:, slots])
+        def hidden_sums(c):
+            z_ps = psum.tile([P, PACK, CHUNK], F32, name="z_ps%d" % c, tag="bank%d" % c)
+            for t in (range(PACK) if c % 2 == 0 else reversed(range(PACK))):
+                cols = slice(t * P, (t + 1) * P)
+                mx_pass(nc, z_ps[:, t, :], wa_codes[:, cols].bitcast(FP8X4), wa_sc[:, cols], tok_codes[c // 2][:, (c % 2) * CHUNK : (c % 2 + 1) * CHUNK].bitcast(FP4X4), tok_sc[:, c * CHUNK : (c + 1) * CHUNK])
+            return z_ps[:].rearrange("p t n -> p n t")
 
-        x_early = held.tile([P, HALF], F32, name="x_early")
-        nc.vector.tensor_tensor(x_early[:], high_ps[:, :HALF], rw_all[:, :HALF], MULT)
-        x_late = held.tile([P, HALF], F32, name="x_late")
-        nc.vector.tensor_tensor(x_late[:], high_ps[:, HALF:], rw_all[:, HALF:], MULT)
-        nc.vector.tensor_copy(windows[1][:].indirect(offsets[:, : HALF // 16]), x_early[:])
-        nc.scalar.activation(windows[1][:].indirect(offsets[:, HALF // 16 :]), x_late[:], COPY)
+        def quantise_hidden(c, h_bf):
+            nc.vector.quantize_mx(out=h_codes[c // 2][:, (c % 2) * CHUNK : (c % 2 + 1) * CHUNK].bitcast(FP8X4), scales=h_sc[:, c * CHUNK : (c + 1) * CHUNK], in_=h_bf[:].rearrange("p n t -> p (n t)"))
+
+        def output_sums(tag, e0, s0, s1):
+            o_ps = psum.tile([P, s1 - s0], F32, name="o_ps_%d_%d" % (e0, s0), tag=tag)
+            mx_pass(nc, o_ps[:], wb_codes[:, e0 : e0 + P].bitcast(FP8X4), wb_sc[:, e0 : e0 + P], h_codes[s0 // HALF][:, s0 % HALF : s0 % HALF + s1 - s0].bitcast(FP8X4), h_sc[:, s0:s1])
+            return o_ps
+
+        h_first = shared.tile([P, HALF], U32, name="h_first", align_bytes=64, offset=WB_AT)
+        h_second = held.tile([P, HALF], U32, name="h_second", align_bytes=64)
+        h_codes = (h_first, h_second)
+        h_sc = held.tile([P, I], U8, name="h_sc", align_bytes=64)
+        x_low = held.tile([P, I], F32, name="x_low")
+        x_high = held.tile([P, I], F32, name="x_high")
+
+        for c in range(3):
+            h_bf = held.tile([P, CHUNK, PACK], BF16, name="h_bf%d" % c, align_bytes=64)
+            nc.scalar.activation(h_bf[:], hidden_sums(c), RELU)
+            if c == 2:
+                last_sums = hidden_sums(3)
+                nc.vector.quantize_mx(out=wb_codes[:, P:].bitcast(FP8X4), scales=wb_sc[:, P:], in_=wb_bf[:, P:].rearrange("p e j -> p (e j)"))
+                for u in range(2):
+                    chunk = slice(u * CHUNK, (u + 1) * CHUNK)
+                    o_ps = output_sums(("rw_ps", "low_a")[u], 0, u * CHUNK, (u + 1) * CHUNK)
+                    nc.vector.tensor_tensor(x_low[:, chunk], o_ps[:], rw_all[:, chunk], MULT)
+                nc.scalar.activation(windows[0][:].indirect(offsets[:, : HALF // 16]), x_low[:, :HALF], COPY)
+                high_first = output_sums("high_a", P, 0, HALF)
+            quantise_hidden(c, h_bf)
+        h_last = shared.tile([P, CHUNK, PACK], BF16, name="h_last", align_bytes=64, offset=WB_AT)
+        nc.vector.tensor_scalar_max(h_last[:], last_sums, 0.0)
+        nc.vector.tensor_tensor(x_high[:, :HALF], high_first[:], rw_all[:, :HALF], MULT)
+        quantise_hidden(3, h_last)
+        for c in (2, 3):
+            chunk = slice(c * CHUNK, (c + 1) * CHUNK)
+            o_ps = output_sums(("bank1", "low_b")[c - 2], 0, c * CHUNK, (c + 1) * CHUNK)
+            nc.vector.tensor_tensor(x_low[:, chunk], o_ps[:], rw_all[:, chunk], MULT)
+        high_second = output_sums("bank0", P, HALF, I)
+        nc.scalar.activation(windows[0][:].indirect(offsets[:, HALF // 16 :]), x_low[:, HALF:], COPY)
+        nc.vector.tensor_tensor(x_high[:, HALF:], high_second[:], rw_all[:, HALF:], MULT)
+        nc.vector.tensor_tensor(windows[1][:].indirect(offsets[:, HIGH_SPLIT // 16 :]), x_high[:, HIGH_SPLIT:], nothing[:], ADD)
+        nc.scalar.activation(windows[1][:].indirect(offsets[:, : HIGH_SPLIT // 16]), x_high[:, :HIGH_SPLIT], COPY)
 
         out_low = held.tile([P, T], F32, name="out_low")
         for c0, c1 in zip(LOW_CUTS, LOW_CUTS[1:]):

@@ -22,13 +22,13 @@ P = 128
 PACK = 4
 CHUNK = 128
 HALF = 256
-WA_SPLIT = 88
+WA_SPLIT = 64
 HIGH_SPLIT = 320
 VECTOR_ZERO_CUTS = (0, 703, 1408)
 GPSIMD_ZERO_PIECES = ((0, 1408, 2048), (1, 0, 768), (1, 768, 1408), (1, 1408, 1792), (1, 1792, 2048))
 LOW_CUTS = (0, 256, 768, 1408, 2048)
 HIGH_CUTS = (0, 640, 1280, 1792, 2048)
-LOW_AT, WA_AT, WB_AT, WORDS_AT, ROUNDED_AT, SCALES_AT = 0, 6144, 14336, 18432, 26624, 30720
+LOW_AT, WA_AT, WB_AT, WORDS_AT, ROUNDED_AT, SCALES_AT = 0, 6144, 14336, 18432, 27136, 31232
 
 
 def mx_pass(nc, out, lhs_codes, lhs_scales, rhs_codes, rhs_scales):
@@ -59,8 +59,9 @@ def tile_attend_depthffn_kernel(tc, tok_words, tok_scales, wa, wb, rw, res, offs
         words = shared.tile([P, T], U16, name="words", align_bytes=64, offset=WORDS_AT)
         nc.sync.dma_start(words[:].bitcast(I32), tok_words[0].bitcast(I32))
 
-        rw_cols = shared.tile([P, PACK], F32, name="rw_cols", align_bytes=64, offset=ROUNDED_AT)
-        nc.scalar.dma_start(rw_cols[:], rw.rearrange("o (p c) -> (o p) c", c=PACK))
+        rw_tile = shared.tile([P, 16], F32, name="rw_tile", offset=ROUNDED_AT - 32)
+        rw_cols = rw_tile[:, :PACK]
+        nc.scalar.dma_start(rw_cols, rw.rearrange("o (p c) -> (o p) c", c=PACK))
         wb_raw = shared.tile([P, PACK * E], F32, name="wb_raw", align_bytes=64, offset=WB_AT)
         nc.sync.dma_start(wb_raw[:], wb.rearrange("(p j) e -> p (j e)", j=PACK))
 
@@ -92,7 +93,7 @@ def tile_attend_depthffn_kernel(tc, tok_words, tok_scales, wa, wb, rw, res, offs
         wa_src = wa_raw[:].rearrange("p (j m t) -> p m t j", j=PACK, t=PACK)
         nc.vector.tensor_copy(wa_dst[:, :WA_SPLIT], wa_src[:, :WA_SPLIT])
         nc.scalar.copy(wa_dst[:, WA_SPLIT:], wa_src[:, WA_SPLIT:])
-        tok_first = shared.tile([P, HALF], U16, name="tok_first", align_bytes=64, offset=WA_AT + 6144)
+        tok_first = shared.tile([P, HALF], U16, name="tok_first", align_bytes=64, offset=ROUNDED_AT - 2 * HALF)
         nc.vector.tensor_copy(tok_first[:], words[:].indirect(offsets[:, : HALF // 16]))
         wa_codes = held.tile([P, F], U32, name="wa_codes", align_bytes=64)
         wa_sc = held.tile([P, F], U8, name="wa_sc", align_bytes=64)

@@ -23,7 +23,7 @@ PACK = 4
 CHUNK = 128
 HALF = 256
 WA_SPLIT = 64
-HIGH_SPLIT = 320
+HIGH_SPLIT = 160
 VECTOR_ZERO_CUTS = (0, 703, 1408)
 GPSIMD_ZERO_PIECES = ((0, 1408, 2048), (1, 0, 768), (1, 768, 1408), (1, 1408, 1792), (1, 1792, 2048))
 LOW_CUTS = (0, 256, 768, 1408, 2048)
@@ -74,8 +74,6 @@ def tile_attend_depthffn_kernel(tc, tok_words, tok_scales, wa, wb, rw, res, offs
             windows.append(w)
         for c0, c1 in zip(VECTOR_ZERO_CUTS, VECTOR_ZERO_CUTS[1:]):
             nc.vector.memset(windows[0][:, c0:c1], 0.0)
-        nothing = held.tile([P, I - HIGH_SPLIT], F32, name="nothing")
-        nc.vector.memset(nothing[:], 0.0)
         for g, c0, c1 in GPSIMD_ZERO_PIECES:
             nc.gpsimd.memset(windows[g][:, c0:c1], 0.0)
 
@@ -155,15 +153,17 @@ def tile_attend_depthffn_kernel(tc, tok_words, tok_scales, wa, wb, rw, res, offs
         nc.vector.tensor_scalar_max(h_last[:], last_sums, 0.0)
         nc.vector.tensor_tensor(x_high[:, :HALF], high_first[:], rw_all[:, :HALF], MULT)
         quantise_hidden(3, h_last)
+        nothing = shared.tile([P, HIGH_SPLIT], F32, name="nothing", align_bytes=64, offset=WB_AT)
+        nc.vector.memset(nothing[:], 0.0)
         for c in (2, 3):
             chunk = slice(c * CHUNK, (c + 1) * CHUNK)
             o_ps = output_sums(("bank1", "low_b")[c - 2], 0, c * CHUNK, (c + 1) * CHUNK)
             nc.vector.tensor_tensor(x_low[:, chunk], o_ps[:], rw_all[:, chunk], MULT)
         high_second = output_sums("bank0", P, HALF, I)
         nc.scalar.activation(windows[0][:].indirect(offsets[:, HALF // 16 :]), x_low[:, HALF:], COPY)
+        nc.vector.tensor_tensor(windows[1][:].indirect(offsets[:, : HIGH_SPLIT // 16]), x_high[:, :HIGH_SPLIT], nothing[:], ADD)
         nc.vector.tensor_tensor(x_high[:, HALF:], high_second[:], rw_all[:, HALF:], MULT)
-        nc.vector.tensor_tensor(windows[1][:].indirect(offsets[:, HIGH_SPLIT // 16 :]), x_high[:, HIGH_SPLIT:], nothing[:], ADD)
-        nc.scalar.activation(windows[1][:].indirect(offsets[:, : HIGH_SPLIT // 16]), x_high[:, :HIGH_SPLIT], COPY)
+        nc.scalar.activation(windows[1][:].indirect(offsets[:, HIGH_SPLIT // 16 :]), x_high[:, HIGH_SPLIT:], COPY)
 
         out_low = held.tile([P, T], F32, name="out_low")
         for c0, c1 in zip(LOW_CUTS, LOW_CUTS[1:]):

@@ -24,8 +24,8 @@ CHUNK = 128
 HALF = 256
 WA_SPLIT = 64
 HIGH_SPLIT = 160
-VECTOR_ZERO_CUTS = (0, 703, 1408)
-GPSIMD_ZERO_PIECES = ((0, 1408, 2048), (1, 0, 768), (1, 768, 1408), (1, 1408, 1792), (1, 1792, 2048))
+VECTOR_ZERO_CUTS = (0, 511, 1024)
+GPSIMD_ZERO_PIECES = ((0, 1024, 1664), (0, 1664, 2048), (1, 0, 1024), (1, 1024, 1664), (1, 1664, 2048))
 LOW_CUTS = (0, 256, 768, 1408, 2048)
 HIGH_CUTS = (0, 640, 1280, 1792, 2048)
 LOW_AT, WA_AT, WB_AT, WORDS_AT, ROUNDED_AT, SCALES_AT = 0, 6144, 14336, 18432, 27136, 31232

@@ -25,7 +25,7 @@ HALF = 256
 WA_SPLIT = 64
 HIGH_SPLIT = 160
 VECTOR_ZERO_CUTS = (0, 511, 1024)
-GPSIMD_ZERO_PIECES = ((0, 1024, 1664), (0, 1664, 2048), (1, 0, 1024), (1, 1024, 1664), (1, 1664, 2048))
+GPSIMD_ZERO_PIECES = ((0, 1024, 1472), (0, 1472, 2048), (1, 0, 1024), (1, 1024, 1664), (1, 1664, 2048))
 LOW_CUTS = (0, 256, 768, 1408, 2048)
 HIGH_CUTS = (0, 640, 1280, 1792, 2048)
 LOW_AT, WA_AT, WB_AT, WORDS_AT, ROUNDED_AT, SCALES_AT = 0, 6144, 14336, 18432, 27136, 31232
@@ -50,8 +50,8 @@ def tile_attend_depthffn_kernel(tc, tok_words, tok_scales, wa, wb, rw, res, offs
 
         wa_raw = shared.tile([P, PACK * F], F32, name="wa_raw", align_bytes=64, offset=WA_AT)
         wa_rows = wa.rearrange("(p j) f -> p (j f)", j=PACK)
-        nc.sync.dma_start(offsets[:], offs)
         nc.sync.dma_start(wa_raw[:, : 2 * F], wa_rows[:, : 2 * F])
+        nc.sync.dma_start(offsets[:], offs)
         scales_by_r = tok_scales[0].bitcast(I32).rearrange("(q r) c -> r q c", r=4)
         for r in range(4):
             nc.sync.dma_start(scale_rows[r:P:32, :].bitcast(I32), scales_by_r[r])
@@ -87,8 +87,8 @@ def tile_attend_depthffn_kernel(tc, tok_words, tok_scales, wa, wb, rw, res, offs
         nc.vector.tensor_copy(tok_sc[:], scale_rows[:].indirect(offsets[:]))
 
         wa_bf = shared.tile([P, PACK, P, PACK], BF16, name="wa_bf", align_bytes=64, offset=ROUNDED_AT)
-        wa_dst = wa_bf[:].rearrange("p t m j -> p m t j")
-        wa_src = wa_raw[:].rearrange("p (j m t) -> p m t j", j=PACK, t=PACK)
+        wa_dst = wa_bf[:].rearrange("p t m j -> p m j t")
+        wa_src = wa_raw[:].rearrange("p (j m t) -> p m j t", j=PACK, t=PACK)
         nc.vector.tensor_copy(wa_dst[:, :WA_SPLIT], wa_src[:, :WA_SPLIT])
         nc.scalar.copy(wa_dst[:, WA_SPLIT:], wa_src[:, WA_SPLIT:])
         tok_first = shared.tile([P, HALF], U16, name="tok_first", align_bytes=64, offset=ROUNDED_AT - 2 * HALF)

@@ -22,6 +22,7 @@ P = 128
 PACK = 4
 CHUNK = 128
 HALF = 256
+WA_FIRST = 1280
 WA_SPLIT = 64
 HIGH_SPLIT = 160
 VECTOR_ZERO_CUTS = (0, 511, 1024)
@@ -50,12 +51,12 @@ def tile_attend_depthffn_kernel(tc, tok_words, tok_scales, wa, wb, rw, res, offs
 
         wa_raw = shared.tile([P, PACK * F], F32, name="wa_raw", align_bytes=64, offset=WA_AT)
         wa_rows = wa.rearrange("(p j) f -> p (j f)", j=PACK)
-        nc.sync.dma_start(wa_raw[:, : 2 * F], wa_rows[:, : 2 * F])
+        nc.sync.dma_start(wa_raw[:, : WA_FIRST], wa_rows[:, : WA_FIRST])
         nc.sync.dma_start(offsets[:], offs)
         scales_by_r = tok_scales[0].bitcast(I32).rearrange("(q r) c -> r q c", r=4)
         for r in range(4):
             nc.sync.dma_start(scale_rows[r:P:32, :].bitcast(I32), scales_by_r[r])
-        nc.sync.dma_start(wa_raw[:, 2 * F :], wa_rows[:, 2 * F :])
+        nc.sync.dma_start(wa_raw[:, WA_FIRST:], wa_rows[:, WA_FIRST:])
         words = shared.tile([P, T], U16, name="words", align_bytes=64, offset=WORDS_AT)
         nc.sync.dma_start(words[:].bitcast(I32), tok_words[0].bitcast(I32))
 

@@ -23,7 +23,7 @@ PACK = 4
 CHUNK = 128
 HALF = 256
 WA_FIRST = 1280
-WA_SPLIT = 64
+WA_SPLIT = 80
 HIGH_SPLIT = 160
 VECTOR_ZERO_CUTS = (0, 511, 1024)
 GPSIMD_ZERO_PIECES = ((0, 1024, 1472), (0, 1472, 2048), (1, 0, 1024), (1, 1024, 1664), (1, 1664, 2048))

from contextlib import ExitStack

import concourse.mybir as mybir

K, T, I, F, E = 512, 2048, 512, 512, 256
FLOPS = 2 * K * F * I + 2 * F * E * I

F32 = mybir.dt.float32
BF16 = mybir.dt.bfloat16
I32 = mybir.dt.int32
U32 = mybir.dt.uint32
U16 = mybir.dt.uint16
U8 = mybir.dt.uint8
FP8X4 = mybir.dt.float8_e4m3fn_x4
FP4X4 = mybir.dt.float4_e2m1fn_x4
MULT = mybir.AluOpType.mult
ADD = mybir.AluOpType.add
RELU = mybir.ActivationFunctionType.Relu
COPY = mybir.ActivationFunctionType.Copy

P = 128
PACK = 4
CHUNK = 128
HALF = 256
WA_FIRST = 1280
WA_SPLIT = 80
HIGH_SPLIT = 160
VECTOR_ZERO_CUTS = (0, 511, 1024)
GPSIMD_ZERO_PIECES = ((0, 1024, 1472), (0, 1472, 2048), (1, 0, 1024), (1, 1024, 1664), (1, 1664, 2048))
LOW_CUTS = (0, 256, 768, 1408, 2048)
HIGH_CUTS = (0, 640, 1280, 1792, 2048)
LOW_AT, WA_AT, WB_AT, WORDS_AT, ROUNDED_AT, SCALES_AT = 0, 6144, 14336, 18432, 27136, 31232


def mx_pass(nc, out, lhs_codes, lhs_scales, rhs_codes, rhs_scales):
    nc.tensor.matmul_mx(out=out, lhsT=lhs_codes, lhsT_scale=lhs_scales, rhs=rhs_codes, rhs_scale=rhs_scales, start=True, stop=True)


def tile_attend_depthffn_kernel(tc, tok_words, tok_scales, wa, wb, rw, res, offs, out):
    nc = tc.nc
    with ExitStack() as ctx:
        held = ctx.enter_context(tc.tile_pool(name="held", bufs=1))
        shared = ctx.enter_context(tc.tile_pool(name="shared", bufs=1))
        psum = ctx.enter_context(tc.psum_pool(name="psum", bufs=1))

        offsets = held.tile([P, I // 16], U16, name="offsets")
        scale_rows = shared.tile([P, T], U8, name="scale_rows", align_bytes=64, offset=SCALES_AT)
        nc.vector.memset(scale_rows[:].bitcast(I32), 0)
        zeros = held.tile([P, P], F32, name="zeros")
        nc.vector.memset(zeros[:], 0.0)

        wa_raw = shared.tile([P, PACK * F], F32, name="wa_raw", align_bytes=64, offset=WA_AT)
        wa_rows = wa.rearrange("(p j) f -> p (j f)", j=PACK)
        nc.sync.dma_start(wa_raw[:, : WA_FIRST], wa_rows[:, : WA_FIRST])
        nc.sync.dma_start(offsets[:], offs)
        scales_by_r = tok_scales[0].bitcast(I32).rearrange("(q r) c -> r q c", r=4)
        for r in range(4):
            nc.sync.dma_start(scale_rows[r:P:32, :].bitcast(I32), scales_by_r[r])
        nc.sync.dma_start(wa_raw[:, WA_FIRST:], wa_rows[:, WA_FIRST:])
        words = shared.tile([P, T], U16, name="words", align_bytes=64, offset=WORDS_AT)
        nc.sync.dma_start(words[:].bitcast(I32), tok_words[0].bitcast(I32))

        rw_tile = shared.tile([P, 16], F32, name="rw_tile", offset=ROUNDED_AT - 32)
        rw_cols = rw_tile[:, :PACK]
        nc.scalar.dma_start(rw_cols, rw.rearrange("o (p c) -> (o p) c", c=PACK))
        wb_raw = shared.tile([P, PACK * E], F32, name="wb_raw", align_bytes=64, offset=WB_AT)
        nc.sync.dma_start(wb_raw[:], wb.rearrange("(p j) e -> p (j e)", j=PACK))

        ident = held.tile([P, P], F32, name="ident")
        nc.gpsimd.affine_select(out=ident[:], in_=zeros[:], compare_op=mybir.AluOpType.not_equal, fill=1.0, base=0, pattern=[[-1, P]], channel_multiplier=1)

        windows = []
        for g in range(2):
            w = held.tile([P, T], F32, name="window%d" % g)
            windows.append(w)
        for c0, c1 in zip(VECTOR_ZERO_CUTS, VECTOR_ZERO_CUTS[1:]):
            nc.vector.memset(windows[0][:, c0:c1], 0.0)
        for g, c0, c1 in GPSIMD_ZERO_PIECES:
            nc.gpsimd.memset(windows[g][:, c0:c1], 0.0)

        rw_ps = psum.tile([P, PACK, P], F32, name="rw_ps", tag="rw_ps")
        for c in range(PACK):
            nc.tensor.transpose(rw_ps[:, c, :], rw_cols[:, c : c + 1].to_broadcast([P, P]), ident[:])
        rw_all = held.tile([P, I], F32, name="rw_all")
        nc.scalar.activation(rw_all[:].rearrange("p (n c) -> p n c", c=PACK), rw_ps[:].rearrange("p c n -> p n c"), COPY)

        tok_sc = held.tile([P, I], U8, name="tok_sc", align_bytes=64)
        nc.vector.tensor_copy(tok_sc[:], scale_rows[:].indirect(offsets[:]))

        wa_bf = shared.tile([P, PACK, P, PACK], BF16, name="wa_bf", align_bytes=64, offset=ROUNDED_AT)
        wa_dst = wa_bf[:].rearrange("p t m j -> p m j t")
        wa_src = wa_raw[:].rearrange("p (j m t) -> p m j t", j=PACK, t=PACK)
        nc.vector.tensor_copy(wa_dst[:, :WA_SPLIT], wa_src[:, :WA_SPLIT])
        nc.scalar.copy(wa_dst[:, WA_SPLIT:], wa_src[:, WA_SPLIT:])
        tok_first = shared.tile([P, HALF], U16, name="tok_first", align_bytes=64, offset=ROUNDED_AT - 2 * HALF)
        nc.vector.tensor_copy(tok_first[:], words[:].indirect(offsets[:, : HALF // 16]))
        wa_codes = held.tile([P, F], U32, name="wa_codes", align_bytes=64)
        wa_sc = held.tile([P, F], U8, name="wa_sc", align_bytes=64)
        for t in range(PACK):
            cols = slice(t * P, (t + 1) * P)
            nc.vector.quantize_mx(out=wa_codes[:, cols].bitcast(FP8X4), scales=wa_sc[:, cols], in_=wa_bf[:, t, :, :].rearrange("p m j -> p (m j)"))
        tok_second = shared.tile([P, HALF], U16, name="tok_second", align_bytes=64, offset=WA_AT + 6656)
        nc.vector.tensor_copy(tok_second[:], words[:].indirect(offsets[:, HALF // 16 :]))
        tok_codes = (tok_first, tok_second)

        wb_src = wb_raw[:].rearrange("p (j c i) -> p c j i", j=PACK, i=4)
        wb_bf = shared.tile([P, E, PACK], BF16, name="wb_bf", align_bytes=64, offset=WA_AT + 4096)
        nc.vector.tensor_copy(wb_bf[:].rearrange("p (c i) j -> p c j i", i=4), wb_src)
        wb_codes = held.tile([P, E], U32, name="wb_codes", align_bytes=64)
        wb_sc = held.tile([P, E], U8, name="wb_sc", align_bytes=64)
        nc.vector.quantize_mx(out=wb_codes[:, :P].bitcast(FP8X4), scales=wb_sc[:, :P], in_=wb_bf[:, :P].rearrange("p e j -> p (e j)"))

        res_low = shared.tile([P, T], F32, name="res_low", align_bytes=64, offset=LOW_AT)
        nc.sync.dma_start(res_low[:], res[:P, :])
        res_high = shared.tile([P, T], F32, name="res_high", align_bytes=64, offset=WORDS_AT)
        nc.sync.dma_start(res_high[:], res[P:, :])

        def hidden_sums(c):
            z_ps = psum.tile([P, PACK, CHUNK], F32, name="z_ps%d" % c, tag="bank%d" % c)
            for t in (range(PACK) if c % 2 == 0 else reversed(range(PACK))):
                cols = slice(t * P, (t + 1) * P)
                mx_pass(nc, z_ps[:, t, :], wa_codes[:, cols].bitcast(FP8X4), wa_sc[:, cols], tok_codes[c // 2][:, (c % 2) * CHUNK : (c % 2 + 1) * CHUNK].bitcast(FP4X4), tok_sc[:, c * CHUNK : (c + 1) * CHUNK])
            return z_ps[:].rearrange("p t n -> p n t")

        def quantise_hidden(c, h_bf):
            nc.vector.quantize_mx(out=h_codes[c // 2][:, (c % 2) * CHUNK : (c % 2 + 1) * CHUNK].bitcast(FP8X4), scales=h_sc[:, c * CHUNK : (c + 1) * CHUNK], in_=h_bf[:].rearrange("p n t -> p (n t)"))

        def output_sums(tag, e0, s0, s1):
            o_ps = psum.tile([P, s1 - s0], F32, name="o_ps_%d_%d" % (e0, s0), tag=tag)
            mx_pass(nc, o_ps[:], wb_codes[:, e0 : e0 + P].bitcast(FP8X4), wb_sc[:, e0 : e0 + P], h_codes[s0 // HALF][:, s0 % HALF : s0 % HALF + s1 - s0].bitcast(FP8X4), h_sc[:, s0:s1])
            return o_ps

        h_first = shared.tile([P, HALF], U32, name="h_first", align_bytes=64, offset=WB_AT)
        h_second = held.tile([P, HALF], U32, name="h_second", align_bytes=64)
        h_codes = (h_first, h_second)
        h_sc = held.tile([P, I], U8, name="h_sc", align_bytes=64)
        x_low = held.tile([P, I], F32, name="x_low")
        x_high = held.tile([P, I], F32, name="x_high")

        for c in range(3):
            h_bf = held.tile([P, CHUNK, PACK], BF16, name="h_bf%d" % c, align_bytes=64)
            nc.scalar.activation(h_bf[:], hidden_sums(c), RELU)
            if c == 2:
                last_sums = hidden_sums(3)
                nc.vector.quantize_mx(out=wb_codes[:, P:].bitcast(FP8X4), scales=wb_sc[:, P:], in_=wb_bf[:, P:].rearrange("p e j -> p (e j)"))
                for u in range(2):
                    chunk = slice(u * CHUNK, (u + 1) * CHUNK)
                    o_ps = output_sums(("rw_ps", "low_a")[u], 0, u * CHUNK, (u + 1) * CHUNK)
                    nc.vector.tensor_tensor(x_low[:, chunk], o_ps[:], rw_all[:, chunk], MULT)
                nc.scalar.activation(windows[0][:].indirect(offsets[:, : HALF // 16]), x_low[:, :HALF], COPY)
                high_first = output_sums("high_a", P, 0, HALF)
            quantise_hidden(c, h_bf)
        h_last = shared.tile([P, CHUNK, PACK], BF16, name="h_last", align_bytes=64, offset=WB_AT)
        nc.vector.tensor_scalar_max(h_last[:], last_sums, 0.0)
        nc.vector.tensor_tensor(x_high[:, :HALF], high_first[:], rw_all[:, :HALF], MULT)
        quantise_hidden(3, h_last)
        nothing = shared.tile([P, HIGH_SPLIT], F32, name="nothing", align_bytes=64, offset=WB_AT)
        nc.vector.memset(nothing[:], 0.0)
        for c in (2, 3):
            chunk = slice(c * CHUNK, (c + 1) * CHUNK)
            o_ps = output_sums(("bank1", "low_b")[c - 2], 0, c * CHUNK, (c + 1) * CHUNK)
            nc.vector.tensor_tensor(x_low[:, chunk], o_ps[:], rw_all[:, chunk], MULT)
        high_second = output_sums("bank0", P, HALF, I)
        nc.scalar.activation(windows[0][:].indirect(offsets[:, HALF // 16 :]), x_low[:, HALF:], COPY)
        nc.vector.tensor_tensor(windows[1][:].indirect(offsets[:, : HIGH_SPLIT // 16]), x_high[:, :HIGH_SPLIT], nothing[:], ADD)
        nc.vector.tensor_tensor(x_high[:, HALF:], high_second[:], rw_all[:, HALF:], MULT)
        nc.scalar.activation(windows[1][:].indirect(offsets[:, HIGH_SPLIT // 16 :]), x_high[:, HIGH_SPLIT:], COPY)

        out_low = held.tile([P, T], F32, name="out_low")
        for c0, c1 in zip(LOW_CUTS, LOW_CUTS[1:]):
            nc.vector.tensor_tensor(out_low[:, c0:c1], res_low[:, c0:c1], windows[0][:, c0:c1], ADD)
            nc.sync.dma_start(out[:P, c0:c1], out_low[:, c0:c1])
        out_high = held.tile([P, T], F32, name="out_high")
        for c0, c1 in zip(HIGH_CUTS, HIGH_CUTS[1:]):
            nc.vector.tensor_tensor(out_high[:, c0:c1], res_high[:, c0:c1], windows[1][:, c0:c1], ADD)
            nc.sync.dma_start(out[P:, c0:c1], out_high[:, c0:c1])
